import numpy as np, ml_dtypes
CORES = [16,18,20,22]
N = 4
BF = ml_dtypes.bfloat16
O, S, FB, NB, ST = 2816, 2048, 32, 3, 6
W = O + S; F = FB * NB
def cut(n, p):
    return np.where(np.arange(16)[:, None] < n, p, -1)
def turns():
    return (np.arange(N)[:, None, None, None] + np.arange(F) // FB) % N
def parts(rng):
    lev = rng.integers(-60, 61, (N, 8, 1, W)) + rng.choice(np.array([-20, 0, 20]), (N, 8, 1, 1))
    D = np.clip(lev + rng.integers(-36, 37, (N, 8, 16, W)), -96, 96)
    x = rng.integers(0, W, (N, 8, 8, 2, O))
    v = rng.integers(0, 4, (N, 8, 16, F)) * (rng.random((N, 8, 1, F)) > 0.05)
    u = rng.random((N, 8, 16, F)); k = rng.integers(0, S, u.shape)
    p = np.where(u < 0.5, rng.integers(0, O, u.shape), O + np.where(u < 0.85, turns(), rng.integers(0, N, u.shape)) * S + k)
    return D, x, v, cut(rng.integers(0, 13, (N, 8, 1, F)), p)
def mend(x):
    c = np.arange(O); a, b = x[:, :, :, 0], x[:, :, :, 1]
    for _ in range(4): a = np.where((a == c) | (a == O + c), (a + 1) % W, a)
    for _ in range(4): b = np.where((b == c) | (b == O + c) | (b == a), (b + 1) % W, b)
    return np.stack([a, b], axis=3)
def pack(D, x, v, p):
    return {"dn": np.ascontiguousarray(D.reshape(N, 128, W)).astype(np.float32).astype(BF), "det": np.ascontiguousarray(mend(x).reshape(N, 128, O)).astype(np.int32),
            "fv": np.ascontiguousarray(v.reshape(N, 128, F)).astype(np.float32).astype(BF), "pth": np.ascontiguousarray(p.reshape(N, 128, F)).astype(np.int32)}
def setup_inputs(rng):
    D, x, v, p = parts(rng)
    return pack(D, x, v, p)
def setup_inputs_ties(rng):
    D, x, v, p = parts(rng); z = np.zeros((1, 1, 16, 1), np.int64)
    D = rng.integers(-3, 4, (N, 8, 1, W)) + z; v = rng.integers(1, 4, (N, 8, 1, F)) + z
    v[:, 1::2] = v[:, 1::2] * (np.arange(16)[:, None] == rng.integers(0, 16, (N, 4, 1, F)))
    x[:, 7, :, 0] = x[:, 7, :, 0] // 2 * 2; x[:, 7, :, 1] = x[:, 7, :, 1] // 2 * 2 + 1
    D[:, 7] = np.where(np.arange(W) % 2 == 1, 3, -3)
    return pack(D, x, v, p)
def setup_inputs_crowd(rng):
    D, x, v, p = parts(rng)
    pool = np.argsort(rng.random((N, 8, W)), axis=-1)[..., :400]; size = np.array([24, 400, 24, 400, 60, 400, 24, 200])[None, :, None]
    x = np.take_along_axis(pool, (rng.random((N, 8, 16 * O)) * size).astype(np.int64), 2).reshape(N, 8, 8, 2, O)
    few = rng.integers(0, O, (N, 8, 10)); np.put_along_axis(D, few[:, :, None, :], 90, 3)
    hot = np.take_along_axis(few, rng.integers(0, 10, (N, 8, 16 * F)), 2).reshape(N, 8, 16, F)
    m = (p >= 0) & (rng.random(p.shape) < np.array([0.7, 0.2, 0.5, 0.1, 0.9, 0.3, 0.4, 0.6])[None, :, None, None])
    return pack(D, x, v, np.where(m, hot, p))
def setup_inputs_full(rng):
    D, x, v, p = parts(rng); v[:, :, 0] = np.maximum(v[:, :, 0], 1); V = (ST + NB - 1) // NB
    for g in range(8):
        d = D[:, g]; xa, xb = x[:, g, :, 0], x[:, g, :, 1]
        if g % 4 == 0:
            z = rng.permutation(S)[:3 * FB * ST].reshape(3, ST, FB)
            d[:, :, O + z[0].reshape(-1)] = 96; d[:, :, O + z[1:].reshape(-1)] = -96
            for t in range(ST):
                xa[:, 0][:, z[0, t]] = O + z[1, t]; xb[:, 0][:, z[0, t]] = O + z[2, t]; b = t % NB
                for n in range(N): p[n, g, t // NB, b * FB:(b + 1) * FB] = O + ((n + t) % N) * S + z[0, t]
        elif g % 4 == 1:
            z = rng.permutation(O); e = z[:(V + 1) * F].reshape(V + 1, F); a = z[(V + 1) * F:(2 * V + 1) * F].reshape(V, F); dead = z[(2 * V + 1) * F:(2 * V + 1) * F + 64]
            v[:, g] = 3 * (v[:, g] > 0)
            d[:, :, e[0]] = 96; d[:, :, a.reshape(-1)] = -96; d[:, :, dead] = -96
            for u in range(V):
                d[:, :, e[u + 1]] = -(u + 1); xa[:, :, e[u]] = a[u]; xb[:, :, e[u]] = e[u + 1]
            p[:, g, :11] = rng.choice(dead, (N, 11, F)); p[:, g, 11] = e[0]; p[:, g, 12:] = -1
        elif g % 4 == 2:
            z = rng.permutation(S); y = z[:3 * F].reshape(3, NB, FB); dead = z[3 * F:3 * F + 64]
            d[:, :, O + y[0].reshape(-1)] = 96; d[:, :, O + y[1:].reshape(-1)] = -96; d[:, :, O + dead] = -96
            p[:, g, 12:] = -1
            for b in range(NB):
                xa[:, 0][:, y[0, b]] = O + y[1, b]; xb[:, 0][:, y[0, b]] = O + y[2, b]
                for n in range(N):
                    s = O + ((n + b) % N) * S
                    p[n, g, :11, b * FB:(b + 1) * FB] = s + rng.choice(dead, (11, FB)); p[n, g, 11, b * FB:(b + 1) * FB] = s + y[0, b]
        else:
            base = O if g == 7 else 0; z = rng.permutation(S)[:3 * FB].reshape(3, FB); w = np.where(rng.permutation(16) < 4, 96, -96)[:, None]
            v[:, g] = 3; p[:, g] = -1
            d[:, :, base + z[0]] = -w; d[:, :, base + z[1]] = w; d[:, :, base + z[2]] = -96
            xa[:, :, z[0]] = base + z[1]; xb[:, :, z[0]] = base + z[2]
            for t in range(ST):
                b = t % NB
                for n in range(N): p[n, g, t // NB, b * FB:(b + 1) * FB] = z[0] + (O + ((n + t) % N) * S if g == 7 else 0)
    return pack(D, x, v, p)
def setup_inputs_ends(rng):
    D, x, v, p = parts(rng); e = np.array([0, O - 1, O, W - 1])
    D[..., e] = rng.choice(np.array([-96, 96]), (N, 8, 1, 4)); x[:, ::2] = rng.choice(e, (N, 4, 8, 2, O))
    s = O + turns() * S; nxt = O + ((turns() + 1) % N) * S; prv = O + ((turns() - 1) % N) * S + S - 1; j = rng.integers(0, 7, p.shape)
    o = np.where(j == 0, 0, np.where(j == 1, O - 1, np.where(j == 2, s, np.where(j == 3, s + S - 1, np.where(j == 5, nxt, np.where(j == 6, prv, O + N * S - 1))))))
    p = cut(rng.choice(np.array([0, 1, 12]), (N, 8, 1, F)), np.where(rng.random(p.shape) < 0.6, o, rng.integers(0, O + N * S, p.shape)))
    v = 3 * rng.integers(0, 2, (N, 8, 1, F)) + np.zeros((1, 1, 16, 1), np.int64)
    D[rng.integers(0, N), 3] = -96; p[:, 5] = -1
    return pack(D, x, v, p)
def setup_inputs_spread(rng):
    D, x, v, p = parts(rng)
    D = np.clip(np.rint(np.exp2(6.6 * rng.random((N, 8, 1, W))) * (2 * rng.random((N, 8, 16, W)) - 1)), -96, 96)
    v = (rng.random((N, 8, 16, F)) < rng.random((N, 8, 1, F))) * rng.integers(1, 4, (N, 8, 16, F))
    return pack(D, x, v, p)
def check_inputs(d):
    bad = []
    for k, lo, hi in (("dn", -96, 96), ("fv", 0, 3)):
        w = np.asarray(d[k]).astype(np.float32)
        if not np.all((w == np.rint(w)) & (w >= lo) & (w <= hi)): bad.append("whole numbers and range of " + k)
    for k, lo, hi in (("det", 0, W - 1), ("pth", -1, O + N * S - 1)):
        if np.min(d[k]) < lo or np.max(d[k]) > hi: bad.append("range of " + k)
    x = np.asarray(d["det"]).reshape(N, 8, 8, 2, O); a, b, c = x[:, :, :, 0], x[:, :, :, 1], np.arange(O)
    if np.any((a == b) | (a == c) | (a == O + c) | (b == c) | (b == O + c)): bad.append("a detour's links differ from each other, from c and from O + c")
    q = np.asarray(d["pth"]).reshape(N, 8, 16, F) >= 0
    if np.any(q[:, :, 1:] & ~q[:, :, :-1]): bad.append("a path's links come before its empty rows")
    if np.any(q[:, :, 12:]): bad.append("at most 12 links a path")
    return bad
def reference(dn, det, fv, pth):
    D = dn.astype(np.float32).astype(np.int32).reshape(N, 8, 16, W)
    own = D[..., :O].copy(); blk = D[..., O:].copy()
    v = fv.astype(np.float32).astype(np.int32).reshape(N, 8, 16, F)
    p = pth.astype(np.int64).reshape(N, 8, 16, F); dd = det.astype(np.int64).reshape(N, 8, 16, O)
    lower = np.arange(FB)[None, :] < np.arange(FB)[:, None]
    gi, fi = np.arange(8)[:, None], np.arange(FB)[None, :]
    for t in range(ST):
        lo = (t % NB) * FB
        for r in range(N):
            B = (r + t) % N
            win = np.concatenate([own[r], blk[B]], axis=2)
            f = v[r, :, :, lo:lo + FB]; q = p[r, :, :, lo:lo + FB]
            mine = (q >= 0) & (q < O); turn = (q >= O + B * S) & (q < O + (B + 1) * S)
            col = np.where(mine, q, np.where(turn, q - B * S, 0)); site = np.where(col < O, col, col - O)
            ab = np.take_along_axis(dd[r], site.reshape(8, 1, 16 * FB), 2)
            Dab = np.take_along_axis(win, ab.reshape(8, 1, -1), 2).reshape(8, 16, 8, 2, 16, FB); ab = ab.reshape(8, 8, 2, 16, FB)
            add = np.add.reduce(np.maximum(Dab + f[:, :, None, None, None, :], 0) - np.maximum(Dab, 0), axis=1)
            Dl = np.take_along_axis(win, col.reshape(8, 1, -1), 2).reshape(8, 16, 16, FB)
            sub = np.add.reduce(np.maximum(Dl, 0) - np.maximum(Dl - f[:, :, None, :], 0), axis=1)
            sc = np.where((mine | turn)[:, None], add[:, :, 0] + add[:, :, 1] - sub[:, None], 10 ** 6)
            sc = sc.transpose(0, 3, 2, 1).reshape(8, FB, 128)
            best = np.argmin(sc, axis=2); cho = np.min(sc, axis=2) < 0; row, k = best >> 3, best & 7
            nm = np.stack([col[gi, row, fi], ab[gi, k, 0, row, fi], ab[gi, k, 1, row, fi]], axis=2)
            same = np.any(nm[:, :, None, :, None] == nm[:, None, :, None, :], axis=(3, 4))
            com = cho & ~np.any(same & lower[None] & cho[:, None, :], axis=2)
            g, j = np.nonzero(com); l, a, b = nm[g, j, 0], nm[g, j, 1], nm[g, j, 2]; df = f[g, :, j]
            win[g, :, l] -= df; win[g, :, a] += df; win[g, :, b] += df
            n = np.count_nonzero(q >= 0, axis=1)
            q[g, row[g, j], j] = np.where(a < O, a, a + B * S); q[g, n[g, j], j] = np.where(b < O, b, b + B * S)
            own[r] = win[..., :O]; blk[B] = win[..., O:]
    yd = np.stack([np.concatenate([own[r], blk[(r + ST - 1) % N]], axis=2) for r in range(N)])
    return {"yd": yd.reshape(N, 128, W).astype(np.float32).astype(BF), "yp": p.reshape(N, 128, F).astype(np.float32)}

@@ -1,0 +1,511 @@
+from concourse.mybir import AluOpType, AxisListType, ActivationFunctionType
+
+O, S, FB, ST, NR = 2816, 2048, 32, 6, 4
+W = O + S
+P0 = 128
+SB = 2 * (P0 + O)
+DW = SB + ST * S
+BIG = 8192.0
+WT = 1024.0
+XS = 208
+MS = 104
+
+SCRATCH = {
+    "D": ("sbuf", [128, DW], "bfloat16"), "NN": ("sbuf", [128, DW], "float32"),
+    "dets": ("sbuf", [128, O], "int32"), "detf": ("sbuf", [128, O], "float32"),
+    "pi": ("sbuf", [128, 96], "int32"), "ff": ("sbuf", [128, 192], "bfloat16"),
+    "qq": ("sbuf", [128, 96], "float32"), "ypo": ("sbuf", [128, 96], "float32"),
+    "X": ("sbuf", [128, 32 * XS], "bfloat16"), "XL": ("sbuf", [128, 512], "bfloat16"),
+    "fexp": ("sbuf", [128, 1536], "bfloat16"), "delta": ("sbuf", [128, 288], "bfloat16"),
+    "abf": ("sbuf", [128, 1536], "float32"), "ab16": ("sbuf", [128, 1536], "uint16"),
+    "GG": ("sbuf", [128, 288], "float32"), "offL": ("sbuf", [128, 96], "uint16"), "site": ("sbuf", [128, 96], "uint16"),
+    "WW": ("sbuf", [128, 192], "float32"), "tp": ("sbuf", [128, 512], "float32"),
+    "ci": ("sbuf", [128, 768], "float32"), "c2": ("sbuf", [128, 464], "float32"), "pint": ("sbuf", [128, 8], "int32"),
+    "col": ("sbuf", [128, 16], "float32"),
+    "identf": ("sbuf", [128, 128], "float32"), "identb": ("sbuf", [128, 128], "bfloat16"), "blockf": ("sbuf", [128, 128], "float32"),
+    "Zp": ("sbuf", [128, 144], "bfloat16"), "Zn": ("sbuf", [128, 144], "bfloat16"),
+    "maskT": ("sbuf", [128, 48], "float32"), "cscan": ("sbuf", [128, 48], "float32"), "i16": ("sbuf", [128, 48], "float32"),
+    "MW": ("sbuf", [128, 768], "float32"), "lowc": ("sbuf", [128, 224], "bfloat16"),
+    "oc": ("sbuf", [128, 144], "uint16"), "tr": ("sbuf", [128, 8], "bfloat16"), "c4": ("sbuf", [128, 4], "float32"),
+    "Lsb": ("sbuf", [128, 32], "bfloat16"),
+    "key": ("sbuf", [128, 8], "float32"), "u": ("sbuf", [128, 16], "int32"), "o16": ("sbuf", [128, 32], "uint16"),
+    "M": ("sbuf", [128, 96], "float32"), "XO": ("sbuf", [128, 96], "float32"), "ne": ("sbuf", [128, 288], "bfloat16"),
+    "ns": ("sbuf", [128, 288], "bfloat16"), "nd": ("sbuf", [128, 96], "float32"), "nn": ("sbuf", [128, 96], "float32"),
+    "rd": ("sbuf", [128, 96], "float32"),
+    "yy": ("sbuf", [128, 32], "float32"), "ncd": ("sbuf", [128, 32], "float32"), "oo": ("sbuf", [128, 8], "uint16"),
+    "mo": ("sbuf", [128, 10 * MS], "uint16"), "lo": ("sbuf", [128, 10 * MS], "uint16"),
+    "S0": ("psum", [128, 512], "float32"), "S1": ("psum", [128, 512], "float32"), "PL": ("psum", [128, 512], "float32"),
+    "NA": ("psum", [128, 512], "float32"), "NB": ("psum", [128, 512], "float32"), "PB": ("psum", [128, 512], "float32"),
+    "PC": ("psum", [128, 512], "float32"),
+}
+PSUM = ("S0", "S1", "PL", "NA", "NB", "PB", "PC")
+SEMAPHORES = (["qv", "qa", "qp", "qg", "ml"] + ["ld%d" % k for k in range(7)] + ["st%d" % k for k in range(3)]
+              + ["ba%d" % k for k in range(5)] + ["ma%d" % k for k in range(10)] + ["bl%d" % k for k in range(5)])
+
+NA0 = [9, 9, 9, 9, 9, 9]
+NA1 = [12, 12, 12, 12, 12, 12]
+KEEP = [0, 5, 5, 5, 5]
+LP, FL, GAPS, PRE = 7, (7,), (0, 1, 2, 7), 2
+add, sub, mul, mx, mn = AluOpType.add, AluOpType.subtract, AluOpType.mult, AluOpType.max, AluOpType.min
+eq, neq, ge, gt = AluOpType.is_equal, AluOpType.not_equal, AluOpType.is_ge, AluOpType.is_gt
+AF = ActivationFunctionType
+
+
+def rank_program(g, core, T, topo):
+    r = T.rank_of(core)
+    if r is None:
+        return
+    Q = {"v": g.vector, "a": g.scalar, "p": g.tensor, "g": g, "s": g.sync}
+    cnt = {"qv": 0, "qa": 0, "qp": 0, "qg": 0}
+    known = {q: {} for q in Q}
+    hist = {}
+    final = {}
+
+    def V(name, lo, hi, step=1):
+        return (T[name][:, lo:hi:step] if step > 1 else T[name][:, lo:hi], [(name, lo, hi)])
+
+    def I(win, off):
+        return (win[0].indirect(off[0]), win[1], off[1])
+
+    def ap(x):
+        return x[0] if isinstance(x, tuple) else x
+
+    def wait(q, toks):
+        for tk in sorted(toks, key=lambda z: -z[1]):
+            if known[q].get(tk[0], 0) < tk[1]:
+                Q[q].wait_ge(T.sem[tk[0]], tk[1])
+                known[q][tk[0]] = tk[1]
+                for k, v in tk[2].items():
+                    if known[q].get(k, 0) < v:
+                        known[q][k] = v
+
+    def note(q, tk, rd, wr):
+        for lst, w in ((rd, False), (wr, True)):
+            for nm, lo, hi in lst:
+                h = hist.setdefault(nm, [])
+                if w:
+                    h[:] = [e for e in h if not (lo <= e[0] and e[1] <= hi and nm not in PSUM)]
+                h[:] = [e for e in h if not (e[4] == q and e[3][0] == tk[0] and lo <= e[0] and e[1] <= hi and (w or not e[2]))]
+                h.append((lo, hi, w, tk, q))
+        final[tk[0]] = max(final.get(tk[0], 0), tk[1])
+
+    def op(q, fn, ins, outs, sem=None, inc=1, extra=()):
+        rd, wr = [], []
+        for x in ins:
+            if isinstance(x, tuple):
+                for part in x[1:]:
+                    rd += part
+        for x in outs:
+            wr += x[1]
+            for part in x[2:]:
+                rd += part
+        who = sem or q
+        toks = list(extra)
+        for lst, w in ((rd, False), (wr, True)):
+            for nm, lo, hi in lst:
+                for e in hist.get(nm, []):
+                    if nm in PSUM and e[4] != who:
+                        toks.append(e[3])
+                    elif (w or e[2]) and lo < e[1] and e[0] < hi and not (who == "p" and e[4] == "p"):
+                        toks.append(e[3])
+        wait(q, toks)
+        if sem is None:
+            sem = "q" + q
+            cnt[sem] += 1
+            tk = (sem, cnt[sem], dict(known[q]))
+            fn().then_inc(T.sem[sem], 1)
+        else:
+            tk = (sem, inc, dict(known[q]))
+            fn()
+        note(who, tk, rd, wr)
+        return tk
+
+    def ts(o, i, s1, op0, s2=None, op1=None):
+        if op1 is None:
+            return op("v", lambda: g.vector.tensor_scalar(o[0], i[0], ap(s1), None, op0), [i, s1], [o])
+        return op("v", lambda: g.vector.tensor_scalar(o[0], i[0], ap(s1), ap(s2), op0, op1), [i, s1, s2], [o])
+
+    def tt(o, a, b, f):
+        return op("v", lambda: g.vector.tensor_tensor(o[0], a[0], b[0], f), [a, b], [o])
+
+    def cp(o, i):
+        return op("v", lambda: g.vector.tensor_copy(o[0], i[0]), [i], [o])
+
+    def ms(o, c):
+        return op("v", lambda: g.vector.memset(o[0], c), [], [o])
+
+    def red(o, i):
+        return op("v", lambda: g.vector.tensor_reduce(o[0], i[0], AxisListType.X, mn), [i], [o])
+
+    def scan(o, d0, d1, ini, op0, op1):
+        return op("v", lambda: g.vector.tensor_tensor_scan(o[0], d0[0], d1[0], ini, op0, op1), [d0, d1], [o])
+
+    def act(o, i, f, bias=None, scale=1.0):
+        if bias is None:
+            return op("a", lambda: g.scalar.activation(o[0], i[0], f, scale=scale), [i], [o])
+        return op("a", lambda: g.scalar.activation(o[0], i[0], f, bias=ap(bias), scale=scale), [i, bias], [o])
+
+    def aff(o, i, a, c, on):
+        return act(o, i, AF.Identity, c, a) if on == "a" else ts(o, i, a, mul, c, add)
+
+    def mm(o, l, x, st, sp):
+        return op("p", lambda: g.tensor.matmul(o[0], l[0], x[0], st, sp), [l, x], [o])
+
+    def iota(o, pat, base=0, cm=0, flt=True):
+        if flt:
+            return op("g", lambda: g.iota(o[0], pat, base, cm, allow_small_or_imprecise_dtypes=True), [], [o])
+        return op("g", lambda: g.iota(o[0], pat, base, cm), [], [o])
+
+    def dma(q, sem, o, i):
+        return op(q, lambda: Q[q].dma_start(o[0], i[0]).then_inc(T.sem[sem], 16), [i], [o], sem=sem, inc=16)
+
+    def H(x):
+        return (x, [])
+
+    def slot(t):
+        return SB + t * S
+
+    def C(k):
+        return V("col", k, k + 1)
+
+    def tp(k, n=1):
+        return V("tp", 32 * k, 32 * (k + n))
+
+    nxt = T.cores[(r - 1) % NR]
+    rid, pid = topo.addr(nxt)[0:2]
+    ne_ = len(topo.engines(core, nxt))
+    m_all = topo.mask(core, nxt)
+    sent = [0]
+
+    def send(src, dst, rsem, lsem, extra=()):
+        if lsem == "ml":
+            sent[0] += ne_
+        op("g", lambda: g.remote_dma(dst[0], src[0], T.sem[rsem], T.sem[lsem], pid, rid, m_all), [src], [],
+           sem=lsem, inc=sent[0] if lsem == "ml" else ne_, extra=extra)
+        note("rem", (rsem, ne_, {}), [], dst[1])
+
+    h = O // 2
+    dma("a", "ld0", V("pi", 0, 96), H(T.pth[:]))
+    dma("s", "ld1", V("ff", 0, 96), H(T.fv[:]))
+    dma("s", "ld2", V("dets", 0, h), H(T.det[:, 0:h]))
+    dma("s", "ld6", V("dets", h, O), H(T.det[:, h:O]))
+    dma("s", "ld3", V("D", SB, SB + S), H(T.dn[:, O:W]))
+    dma("s", "ld4", V("D", P0, P0 + h), H(T.dn[:, 0:h]))
+    last_load = dma("s", "ld5", V("D", P0 + h, P0 + O), H(T.dn[:, h:O]))
+
+    def prep_ops(t, on="a"):
+        b = t % 3
+        B = (r + t) % NR
+        q = V("qq", 32 * b, 32 * b + 32)
+        sh = float(slot(t) - P0 - O)
+        L = [lambda: aff(tp(0), q, 1.0, float(-B * S), on),
+             lambda: ts(tp(2), q, float(P0), mx, float(P0 + O - 1), mn),
+             lambda: act(tp(8), q, AF.Sign, float(1 - P0)) if on == "a" else ts(tp(8), q, float(P0), ge),
+             lambda: tt(tp(4), tp(2), q, eq),
+             lambda: ts(tp(1), tp(0), float(P0 + O), mx, float(P0 + W - 1), mn),
+             lambda: tt(tp(2), tp(2), tp(4), mul),
+             lambda: (mm(V("PC", 0, 32), V("blockf", 0, 128), tp(8), True, True), tt(tp(3), tp(1), tp(0), eq)),
+             lambda: ts(V("WW", 64 * b + 32, 64 * b + 64), V("PC", 0, 32), C(1), eq),
+             lambda: (aff(tp(6), tp(3), float(-O), float(-P0), on), aff(tp(7), tp(3), sh, 0.0, on), tt(tp(1), tp(1), tp(3), mul)),
+             lambda: tt(tp(5), tp(1), tp(2), add),
+             lambda: tt(tp(6), tp(6), tp(5), add),
+             lambda: tt(tp(7), tp(7), tp(5), add),
+             lambda: cp(V("site", 32 * b, 32 * b + 32), tp(6))]
+        for jh in range(2):
+            L.append(lambda jh=jh: (cp(V("offL", 32 * b + jh, 32 * b + 32, 2), V("tp", 224 + 16 * jh, 240 + 16 * jh)),
+                                    aff(V("GG", 96 * b + 48 * jh + 32, 96 * b + 48 * jh + 48), V("tp", 160 + 16 * jh, 176 + 16 * jh), 1.0, 0.0, on)))
+        return L
+
+    iota(V("pint", 0, 1), [[0, 1]], 0, 1, False)
+    iota(V("c2", 144, 272), [[1, 8], [0, 16]])
+    iota(V("c2", 336, 432), [[32, 3], [1, 16], [16, 2]])
+    iota(V("c2", 432, 450), [[16, 6], [0, 3]])
+    iota(V("c2", 0, 144), [[1, 144]])
+    iota(V("c2", 272, 320), [[0, 3], [1, 16]])
+    iota(V("c2", 320, 326), [[16, 6]], 32)
+    iota(V("lowc", 0, 112), [[16, 14], [1, 8]])
+    iota(V("lowc", 112, 224), [[16, 14], [1, 8]])
+    iota(V("ci", 0, 256), [[0, 16], [2, 16]])
+    iota(V("ci", 256, 512), [[0, 16], [2, 16]], 1)
+    iota(V("ci", 512, 768), [[1, 16], [100, 2], [0, 8]])
+    iota(V("D", P0 + O, SB), [[0, P0 + O]])
+    ms(V("D", 0, P0), 0.0)
+    ms(V("NN", 0, P0), 0.0)
+    ms(V("mo", 0, 10 * MS), 0)
+    ms(V("c4", 0, 2), 65536.0)
+    ms(V("c4", 2, 3), 65536.0 + 256)
+    ms(V("c4", 3, 4), 65536.0 + 512)
+    cp(C(0), V("pint", 0, 1))
+    ts(V("pint", 1, 2), V("pint", 0, 1), 15, AluOpType.bitwise_and)
+    ts(V("pint", 2, 3), V("pint", 0, 1), 4, AluOpType.arith_shift_right)
+    cp(V("oc", 0, 96), V("c2", 336, 432))
+    cp(V("col", 1, 3), V("pint", 1, 3))
+    ts(V("c2", 434, 450, 3), V("c2", 434, 450, 3), 96.0, add)
+    ts(V("blockf", 0, 128), V("c2", 144, 272), C(2), eq)
+    ts(V("oc", 96, 114), V("c2", 432, 450), C(1), add)
+    ts(C(3), C(2), 16.0, mul, 15.0, add)
+    ts(C(5), C(1), 16.0, mul)
+    ts(C(6), C(1), 16.0, mul, 256.0, add)
+    ts(V("identf", 0, 128), V("c2", 0, 128), C(0), eq)
+    ts(V("identb", 0, 128), V("c2", 0, 128), C(0), eq)
+    ts(V("Zp", 0, 144), V("c2", 0, 144), C(3), eq, WT, mul)
+    ts(V("Zn", 0, 144), V("c2", 0, 144), C(3), eq, -WT, mul)
+    ts(V("qq", 0, 96), V("pi", 0, 96), float(P0), add)
+    ts(V("ff", 96, 192), V("ff", 0, 96), -1.0, mul)
+    act(V("fexp", 0, 1536), I(V("ff", 0, 96), V("oc", 0, 96)), AF.Copy)
+    act(V("delta", 0, 288), I(V("ff", 0, 192), V("oc", 96, 114)), AF.Copy)
+    more = [lambda: ts(V("i16", 0, 48), V("c2", 272, 320), C(1), eq),
+            lambda: ts(V("maskT", 0, 48), V("c2", 272, 320), C(1), gt),
+            lambda: ts(V("cscan", 0, 48), V("c2", 272, 320), C(1), neq),
+            lambda: ts(V("tr", 0, 6), V("c2", 320, 326), C(1), add),
+            lambda: tt(V("maskT", 0, 48), V("i16", 0, 48), V("maskT", 0, 48), sub),
+            lambda: ms(V("lowc", 96, 97), 232.0 - WT),
+            lambda: ms(V("lowc", 112 + 104, 112 + 105), 232.0 - WT),
+            lambda: ts(V("maskT", 0, 48), V("maskT", 0, 48), BIG, mul)]
+    for k, f in enumerate(prep_ops(0, "v")):
+        f()
+        if k < len(more):
+            more[k]()
+    for f in prep_ops(1, "v"):
+        f()
+    ts(V("detf", 0, h), V("dets", 0, h), float(P0), add)
+    ts(V("abf", 0, 512), I(V("dets", 0, O), V("site", 0, 32)), float(P0), add)
+    ts(V("MW", 0, 768), V("ci", 0, 768), C(1), eq)
+    cp(V("ab16", 0, 512), V("abf", 0, 512))
+    ts(V("detf", h, O), V("dets", h, O), float(P0), add)
+    act(V("NN", P0 + O, P0 + W), V("D", SB, SB + S), AF.Relu, None, -1.0)
+    act(V("NN", P0, P0 + h), V("D", P0, P0 + h), AF.Relu, None, -1.0)
+    hh = P0 + h + 640
+    act(V("NN", P0 + h, hh), V("D", P0 + h, hh), AF.Relu, None, -1.0)
+    ts(V("NN", hh, P0 + O), V("D", hh, P0 + O), -1.0, mul, 0.0, mx)
+
+    def ncol(jh):
+        k = 144 * jh + (71 if jh == 0 else 143)
+        return V("ns", k, k + 1)
+
+    def path_ops(t):
+        b = t % 3
+        B = (r + t) % NR
+        q = V("qq", 32 * b, 32 * b + 32)
+        blk = V("blockf", 0, 128)
+
+        def spread():
+            ts(V("ncd", 16, 32), V("i16", 0, 16), ncol(1), mul)
+            for ty in range(2):
+                for jh in range(2):
+                    mm(V("PB", 32 * ty + 16 * jh, 32 * ty + 16 * jh + 16), blk, V("M", 48 * jh + 16 * ty, 48 * jh + 16 * ty + 16), True, True)
+            for jh in range(2):
+                mm(V("PC", 32 + 16 * jh, 48 + 16 * jh), V("identf", 0, 128), V("M", 48 * jh + 32, 48 * jh + 48), True, True)
+            for k in range(2):
+                mm(V("PB", 64 + 32 * k, 96 + 32 * k), blk, V("ncd", 0, 32), True, True)
+            act(V("WW", 64 * b, 64 * b + 32), V("PC", 32, 64), AF.Sign)
+        L = [lambda: ts(V("ncd", 0, 16), V("i16", 0, 16), ncol(0), mul), spread]
+        L2 = [lambda: ts(tp(10, 2), V("PB", 0, 64), float(P0 + O), ge, float(B * S), mul),
+              lambda: tt(tp(12, 2), V("WW", 64 * b, 64 * b + 64), V("PB", 64, 128), mul),
+              lambda: tt(tp(10, 2), tp(10, 2), V("PB", 0, 64), add),
+              lambda: tt(tp(10), tp(10), q, sub),
+              lambda: tt(tp(10, 2), tp(10, 2), tp(12, 2), mul),
+              lambda: tt(q, q, tp(10), add),
+              lambda: tt(q, q, tp(11), mx)]
+        if t >= 3:
+            L2.append(lambda: aff(V("ypo", 32 * b, 32 * b + 32), q, 1.0, float(-P0), "v" if t == ST - 1 else "a"))
+        return L, L2
+
+    def tail_ops(t, jh):
+        b = t % 3
+        R = 12 if t < 3 else 13
+        sh = float(slot(t) - P0 - O)
+        bank, c0, wd = ("NA", 0, 48) if jh == 0 else ("NB", 48, 96)
+        key = V("key", jh, jh + 1)
+        nc = ncol(jh)
+        u = V("u", 8 * jh, 8 * jh + 4)
+        oS, oK, oD = V("o16", 16 * jh, 16 * jh + 2), V("o16", 16 * jh + 4, 16 * jh + 7), V("o16", 16 * jh + 8, 16 * jh + 11)
+        g0 = 96 * b + 48 * jh
+        Mv = V("M", 48 * jh, 48 * jh + 48)
+        x = V("XO", 48 * jh + 15, 48 * jh + 48, 16)
+        y0 = 16 * jh
+        mk, y, ym = V("yy", y0, y0 + 3), V("yy", y0 + 4, y0 + 7), V("yy", y0 + 8, y0 + 11)
+        nD = V("nd", 48 * jh, 48 * jh + 48)
+        m0 = MS * (2 * t + jh)
+        hw = 3 * wd // 2
+
+        def names():
+            tt(Mv, I(V("MW", 0, 768), oK), V("GG", g0, g0 + 48), mul)
+            mm(V(bank, c0, c0 + 48), V("blockf", 0, 128), Mv, False, True)
+            if jh == 0:
+                mm(V("NB", 0, 48), V("blockf", 0, 128), Mv, True, True)
+                mm(V("NB", 48, 96), V("identf", 0, 128), V("maskT", 0, 48), True, False)
+
+        def cmp_(c):
+            xc = V("XO", 48 * jh + 16 * c + 15, 48 * jh + 16 * c + 16)
+            return lambda: ts(V("ne", wd * c, wd * c + wd), V(bank, 0, wd), BIG, add, xc, neq)
+        L = [lambda: red(key, V("S%d" % jh, 0, 8 * R + 1)),
+             lambda: ts(u, V("c4", 0, 4), key, add),
+             lambda: ts(V("u", 8 * jh + 4, 8 * jh + 8), u, 1023, AluOpType.bitwise_and),
+             lambda: ts(oS, V("u", 8 * jh + 4, 8 * jh + 6), 1.0 / 16, mul, C(5 + jh), add),
+             lambda: cp(oK, V("u", 8 * jh + 5, 8 * jh + 8)),
+             lambda: cp(V("GG", g0, g0 + 32), I(V("abf", 512 * b, 512 * b + 512), oS)),
+             names,
+             lambda: scan(V("XO", 48 * jh, 48 * jh + 48), V("cscan", 0, 48), V(bank, c0, c0 + 48), 0.0, mul, mx),
+             lambda: ts(mk, x, P0 + O + BIG, ge, sh, mul),
+             cmp_(0),
+             lambda: tt(y, x, mk, add),
+             cmp_(1),
+             lambda: ts(oD, y, -BIG, add),
+             cmp_(2),
+             lambda: tt(nD, I(V("D", 0, slot(t) + S), oD), V("delta", g0, g0 + 48), add),
+             lambda: scan(V("ns", 144 * jh, 144 * jh + hw), V("ne", 0, hw), V("ne", hw, 2 * hw), 1.0, mn, mn)]
+        own = []
+        for c in range(3):
+            k = 3 * jh + c
+            ko = k if t < ST - 1 else 4 * jh + c
+            own.append(lambda c=c, k=k, ko=ko: ts(V("oo", ko, ko + 1), V("o16", 16 * jh + 8 + c, 16 * jh + 9 + c), nc, mul, V("tr", k, k + 1), mx))
+        if t == ST - 1:
+            return L + own + [lambda: cp(I(V("D", 0, slot(t) + S), V("oo", 4 * jh, 4 * jh + 3)), nD)], []
+        L.insert(14, lambda: ts(ym, y, -BIG - sh, add))
+        L.append(lambda: ts(V("mo", m0 + 8, m0 + 56), nD, -1.0, mul))
+        L.append(lambda: ts(V("mo", m0 + 56, m0 + 104), nD, 256.0, add))
+        for c in range(3):
+            k = 3 * jh + c
+            L.append(lambda c=c, k=k: ts(V("mo", m0 + c, m0 + c + 1), V("yy", y0 + 8 + c, y0 + 9 + c), nc, mul, V("tr", k, k + 1), mx))
+        L.append(lambda: send(V("mo", m0, m0 + MS), V("lo", m0, m0 + MS), "ma%d" % (2 * t + jh), "ml"))
+        return L, own
+
+    def take(t, jh):
+        m0 = MS * (2 * t + jh)
+        off = V("lo", m0, m0 + 3)
+        return [lambda: cp(I(V("NN", 0, P0 + W), off), V("lo", m0 + 8, m0 + 56)),
+                lambda: ts(V("rd", 48 * jh, 48 * jh + 48), V("lo", m0 + 56, m0 + 104), -256.0, add),
+                lambda: cp(I(V("D", slot(t + 1) - P0 - O, slot(t + 1) + S), off), V("rd", 48 * jh, 48 * jh + 48))]
+
+    def bulk(t):
+        if t < ST - 1:
+            send(V("D", slot(t), slot(t) + S), V("D", slot(t + 1), slot(t + 1) + S), "ba%d" % t, "bl%d" % t, [last_load])
+
+    def detours(t):
+        b = t % 3
+        act(V("abf", 512 * b, 512 * b + 512), I(V("detf", 0, O), V("site", 32 * b, 32 * b + 32)), AF.Copy)
+
+    def narrow(t, k):
+        c = 512 * (t % 3) + 256 * k
+        cp(V("ab16", c, c + 256), V("abf", c, c + 256))
+
+    spill = prep_ops(2)
+    bulk(0)
+    for t in range(ST):
+        b = t % 3
+        R = 12 if t < 3 else 13
+        left = [41, 41]
+        lowv = V("lowc", 0 if R == 12 else 112, 112 if R == 12 else 224)
+
+        def smm(jh, n, l, x, k=0, st=1):
+            left[jh] -= 1
+            mm(V("S%d" % jh, k, n, st), l, x, left[jh] == 40, left[jh] == 0)
+
+        def flow(j, q):
+            jh, j16 = divmod(j, 16)
+            o = V("X", XS * j, XS * j + 16 * R)
+            i = I(V("NN", 0, P0 + W), V("ab16", 512 * b + 16 * j, 512 * b + 16 * j + R))
+            f = V("ff", 32 * b + j, 32 * b + j + 1)
+            if q == "a":
+                act(o, i, AF.Relu, f, -1.0)
+            else:
+                ts(o, i, f, sub, 0.0, mn)
+            z = V("Zp" if q == "a" else "Zn", 15 - j16, 143 - j16)
+            for e in range(2):
+                smm(jh, 8 * R, z, V("X", XS * j + e, XS * j + 16 * R, 2))
+
+        for jh in range(2):
+            smm(jh, 112, V("identb", 0, 128), lowv)
+        mm(V("NA", 0, 48), V("identf", 0, 128), V("maskT", 0, 48), True, False)
+
+        def lrelu():
+            ts(V("XL", 0, 512), V("XL", 0, 512), 0.0, mx)
+            for j16 in range(16):
+                mm(V("PL", 0, 32), V("Zn", 15 - j16, 143 - j16), V("XL", 32 * j16, 32 * j16 + 32), j16 == 0, j16 == 15)
+
+        def lexp():
+            act(V("Lsb", 0, 32), V("PL", 0, 32), AF.Copy)
+            for jh in range(2):
+                for k in range(8):
+                    smm(jh, 8 * R, V("identb", 0, 128), V("Lsb", 16 * jh, 16 * jh + R), k, 8)
+
+        fc = 16 * R * 1.5
+        a0, a1 = NA0[t], NA1[t]
+        t0, t0b = tail_ops(t, 0)
+        t1, t1b = tail_ops(t, 1)
+        A = [(80 + fc, None, "f0", lambda j=j: flow(j, "a")) for j in range(a0)]
+        A[LP:LP] = [(100, "lr", "f0", lexp)]
+        A += [(80 + fc, None, "f1", lambda j=j: flow(j, "a")) for j in range(16, 16 + a1)]
+        fl0 = [(60 + fc, None, "f0", lambda j=j: flow(j, "v")) for j in range(a0, 16)]
+        fl1 = [(60 + fc, None, "f1", lambda j=j: flow(j, "v")) for j in range(16 + a1, 32)]
+        Vq = [(830, None, None, lambda: tt(V("XL", 0, 512), I(V("D", 0, slot(t) + S), V("offL", 32 * b, 32 * b + 32)),
+                                           V("fexp", 512 * b, 512 * b + 512), mn)),
+              fl0.pop(), (260, None, "lr", lrelu)] + fl0
+        small = [(70, None, None, f) for f in spill]
+        for z in range(PRE):
+            Vq.append(fl1.pop())
+        for k, f in enumerate(t0):
+            Vq.append((80, "f0" if k == 0 else None, None, f))
+            if fl1 and (k == 6 or k in FL):
+                Vq.append(fl1.pop())
+            elif k < 9 and small:
+                n = -(-len(small) // (9 - k))
+                Vq += small[:n]
+                small = small[n:]
+        Vq += small + fl1
+        need = {"f0": 17, "lr": 1}
+        tm = {"a": 0.0, "v": 300.0}
+        while A or Vq:
+            q = sorted([q for q, l in (("a", A), ("v", Vq)) if l and need.get(l[0][1], 0) == 0],
+                       key=lambda q: tm[q] + (A if q == "a" else Vq)[0][0])[0]
+            it = (A if q == "a" else Vq).pop(0)
+            it[3]()
+            tm[q] += it[0]
+            if it[2] in need:
+                need[it[2]] -= 1
+        p1, p2 = path_ops(t)
+        if t == ST - 1:
+            p1[0]()
+            for f in t1:
+                f()
+            dma("s", "st0", H(T.yd[:, 0:O]), V("D", P0, P0 + O))
+            dma("a", "st1", H(T.yd[:, O:W]), V("D", slot(t), slot(t) + S))
+            for f in p1[1:] + p2:
+                f()
+            dma("s", "st2", H(T.yp[:]), V("ypo", 0, 96))
+            break
+        act(V("NN", P0 + O, P0 + W), V("D", slot(t + 1), slot(t + 1) + S), AF.Relu, None, -1.0)
+        if t == 0:
+            detours(1)
+        else:
+            narrow(t + 1, 0)
+        k0, k1 = take(t, 0), take(t, 1)
+        gaps = t0b + [p1[0]]
+        for k, f in enumerate(t1):
+            f()
+            if k == 6 and t > 0:
+                narrow(t + 1, 1)
+            elif gaps and (k in GAPS or k == 6):
+                gaps.pop(0)()
+        act(V("nn", 0, 96), V("nd", 0, 96), AF.Relu, None, -1.0)
+        for f in gaps + t1b + p1[1:] + k0[1:2]:
+            f()
+        if t + 2 < ST:
+            detours(t + 2)
+        cp(I(V("D", 0, slot(t) + S), V("oo", 0, 6)), V("nd", 0, 96))
+        if t == 0:
+            narrow(1, 0)
+            narrow(1, 1)
+        cp(I(V("NN", 0, slot(t) + S), V("oo", 0, 6)), V("nn", 0, 96))
+        k0[2]()
+        k0[0]()
+        later = p2 + (prep_ops(t + 3) if t + 3 < ST else [])
+        for f in later[:KEEP[t]]:
+            f()
+        spill = later[KEEP[t]:]
+        for f in k1:
+            f()
+        bulk(t + 1)
+    for sem, v in final.items():
+        g.sync.wait_ge(T.sem[sem], v)

@@ -27,7 +27,7 @@ SCRATCH = {
     "maskT": ("sbuf", [128, 48], "float32"), "cscan": ("sbuf", [128, 48], "float32"), "i16": ("sbuf", [128, 48], "float32"),
     "MW": ("sbuf", [128, 768], "float32"), "lowc": ("sbuf", [128, 224], "bfloat16"),
     "oc": ("sbuf", [128, 144], "uint16"), "tr": ("sbuf", [128, 8], "bfloat16"), "c4": ("sbuf", [128, 4], "float32"),
-    "Lsb": ("sbuf", [128, 32], "bfloat16"),
+    "Lsb": ("sbuf", [128, 32], "bfloat16"), "Lexp": ("sbuf", [128, 224], "bfloat16"),
     "key": ("sbuf", [128, 8], "float32"), "u": ("sbuf", [128, 16], "int32"), "o16": ("sbuf", [128, 32], "uint16"),
     "M": ("sbuf", [128, 96], "float32"), "XO": ("sbuf", [128, 96], "float32"), "ne": ("sbuf", [128, 288], "bfloat16"),
     "ns": ("sbuf", [128, 288], "bfloat16"), "nd": ("sbuf", [128, 96], "float32"), "nn": ("sbuf", [128, 96], "float32"),
@@ -42,10 +42,7 @@ PSUM = ("S0", "S1", "PL", "NA", "NB", "PB", "PC")
 SEMAPHORES = (["qv", "qa", "qp", "qg", "ml"] + ["ld%d" % k for k in range(7)] + ["st%d" % k for k in range(3)]
               + ["ba%d" % k for k in range(5)] + ["ma%d" % k for k in range(10)] + ["bl%d" % k for k in range(5)])
 
-NA0 = [9, 9, 9, 9, 9, 9]
-NA1 = [12, 12, 12, 12, 12, 12]
-KEEP = [0, 5, 5, 5, 5]
-LP, FL, GAPS, PRE = 7, (7,), (0, 1, 2, 7), 2
+PL = {"cyc": 0.9, "gat": 1.4, "sca": 3.5, "pe": 0.6, "lat": 120.0, "rem": 2000.0, "bw": 250.0, "strided": False}
 add, sub, mul, mx, mn = AluOpType.add, AluOpType.subtract, AluOpType.mult, AluOpType.max, AluOpType.min
 eq, neq, ge, gt = AluOpType.is_equal, AluOpType.not_equal, AluOpType.is_ge, AluOpType.is_gt
 AF = ActivationFunctionType
@@ -58,11 +55,14 @@ def rank_program(g, core, T, topo):
     Q = {"v": g.vector, "a": g.scalar, "p": g.tensor, "g": g, "s": g.sync}
     cnt = {"qv": 0, "qa": 0, "qp": 0, "qg": 0}
     known = {q: {} for q in Q}
+    clock = {q: 0.0 for q in Q}
+    clock["dma"] = 0.0
     hist = {}
     final = {}
+    dry = []
 
     def V(name, lo, hi, step=1):
-        return (T[name][:, lo:hi:step] if step > 1 else T[name][:, lo:hi], [(name, lo, hi)])
+        return (T[name][:, lo:hi:step] if step > 1 else T[name][:, lo:hi], [(name, lo, hi, -(-(hi - lo) // step))])
 
     def I(win, off):
         return (win[0].indirect(off[0]), win[1], off[1])
@@ -70,18 +70,19 @@ def rank_program(g, core, T, topo):
     def ap(x):
         return x[0] if isinstance(x, tuple) else x
 
-    def wait(q, toks):
-        for tk in sorted(toks, key=lambda z: -z[1]):
-            if known[q].get(tk[0], 0) < tk[1]:
-                Q[q].wait_ge(T.sem[tk[0]], tk[1])
-                known[q][tk[0]] = tk[1]
-                for k, v in tk[2].items():
-                    if known[q].get(k, 0) < v:
-                        known[q][k] = v
+    def wide(x):
+        return 2 if SCRATCH[x[1][0][0]][2] in ("bfloat16", "uint16") else 4
+
+    def cost(o, i, k=1.0, fix=50.0):
+        if len(o) == 3:
+            return fix + 16 * o[2][0][3] * PL["sca"] * PL["cyc"]
+        if len(i) == 3:
+            return fix + 16 * i[2][0][3] * PL["gat"] * PL["cyc"]
+        return max(64, i[1][0][3] * k * (0.5 if wide(o) + wide(i) == 4 and fix == 50.0 else 1)) * PL["cyc"]
 
     def note(q, tk, rd, wr):
         for lst, w in ((rd, False), (wr, True)):
-            for nm, lo, hi in lst:
+            for nm, lo, hi, n in lst:
                 h = hist.setdefault(nm, [])
                 if w:
                     h[:] = [e for e in h if not (lo <= e[0] and e[1] <= hi and nm not in PSUM)]
@@ -89,7 +90,7 @@ def rank_program(g, core, T, topo):
                 h.append((lo, hi, w, tk, q))
         final[tk[0]] = max(final.get(tk[0], 0), tk[1])
 
-    def op(q, fn, ins, outs, sem=None, inc=1, extra=()):
+    def op(q, fn, ins, outs, c, sem=None, inc=1, extra=()):
         rd, wr = [], []
         for x in ins:
             if isinstance(x, tuple):
@@ -102,62 +103,85 @@ def rank_program(g, core, T, topo):
         who = sem or q
         toks = list(extra)
         for lst, w in ((rd, False), (wr, True)):
-            for nm, lo, hi in lst:
+            for nm, lo, hi, n in lst:
                 for e in hist.get(nm, []):
                     if nm in PSUM and e[4] != who:
                         toks.append(e[3])
                     elif (w or e[2]) and lo < e[1] and e[0] < hi and not (who == "p" and e[4] == "p"):
                         toks.append(e[3])
-        wait(q, toks)
+        start = max([clock[q]] + [tk[3] + PL["lat"] for tk in toks if known[q].get(tk[0], 0) < tk[1]])
+        if dry:
+            dry[0] = (start - clock[q], c, q)
+            raise StopIteration
+        for tk in sorted(toks, key=lambda z: -z[1]):
+            if known[q].get(tk[0], 0) < tk[1]:
+                Q[q].wait_ge(T.sem[tk[0]], tk[1])
+                known[q][tk[0]] = tk[1]
+                for k, v in tk[2].items():
+                    if known[q].get(k, 0) < v:
+                        known[q][k] = v
         if sem is None:
             sem = "q" + q
             cnt[sem] += 1
-            tk = (sem, cnt[sem], dict(known[q]))
+            clock[q] = start + c
+            tk = (sem, cnt[sem], dict(known[q]), clock[q])
             fn().then_inc(T.sem[sem], 1)
         else:
-            tk = (sem, inc, dict(known[q]))
+            clock[q] = start + 100
+            clock["dma"] = max(start + PL["rem"], clock["dma"]) + c
+            tk = (sem, inc, dict(known[q]), clock["dma"])
             fn()
         note(who, tk, rd, wr)
         return tk
 
+    def peek(f):
+        dry.append(None)
+        try:
+            f()
+        except StopIteration:
+            pass
+        return dry.pop()
+
     def ts(o, i, s1, op0, s2=None, op1=None):
         if op1 is None:
-            return op("v", lambda: g.vector.tensor_scalar(o[0], i[0], ap(s1), None, op0), [i, s1], [o])
-        return op("v", lambda: g.vector.tensor_scalar(o[0], i[0], ap(s1), ap(s2), op0, op1), [i, s1, s2], [o])
+            return op("v", lambda: g.vector.tensor_scalar(o[0], i[0], ap(s1), None, op0), [i, s1], [o], cost(o, i))
+        return op("v", lambda: g.vector.tensor_scalar(o[0], i[0], ap(s1), ap(s2), op0, op1), [i, s1, s2], [o], cost(o, i))
 
     def tt(o, a, b, f):
-        return op("v", lambda: g.vector.tensor_tensor(o[0], a[0], b[0], f), [a, b], [o])
+        return op("v", lambda: g.vector.tensor_tensor(o[0], a[0], b[0], f), [a, b], [o], cost(o, a, 2.0))
 
     def cp(o, i):
-        return op("v", lambda: g.vector.tensor_copy(o[0], i[0]), [i], [o])
+        return op("v", lambda: g.vector.tensor_copy(o[0], i[0]), [i], [o], cost(o, i))
 
     def ms(o, c):
-        return op("v", lambda: g.vector.memset(o[0], c), [], [o])
+        return op("v", lambda: g.vector.memset(o[0], c), [], [o], cost(o, o))
 
     def red(o, i):
-        return op("v", lambda: g.vector.tensor_reduce(o[0], i[0], AxisListType.X, mn), [i], [o])
+        return op("v", lambda: g.vector.tensor_reduce(o[0], i[0], AxisListType.X, mn), [i], [o], cost(o, i))
 
     def scan(o, d0, d1, ini, op0, op1):
-        return op("v", lambda: g.vector.tensor_tensor_scan(o[0], d0[0], d1[0], ini, op0, op1), [d0, d1], [o])
+        return op("v", lambda: g.vector.tensor_tensor_scan(o[0], d0[0], d1[0], ini, op0, op1), [d0, d1], [o], cost(o, d0))
 
     def act(o, i, f, bias=None, scale=1.0):
         if bias is None:
-            return op("a", lambda: g.scalar.activation(o[0], i[0], f, scale=scale), [i], [o])
-        return op("a", lambda: g.scalar.activation(o[0], i[0], f, bias=ap(bias), scale=scale), [i, bias], [o])
+            return op("a", lambda: g.scalar.activation(o[0], i[0], f, scale=scale), [i], [o], cost(o, i, 1.0, 65.0))
+        return op("a", lambda: g.scalar.activation(o[0], i[0], f, bias=ap(bias), scale=scale), [i, bias], [o], cost(o, i, 1.0, 65.0))
 
     def aff(o, i, a, c, on):
         return act(o, i, AF.Identity, c, a) if on == "a" else ts(o, i, a, mul, c, add)
 
     def mm(o, l, x, st, sp):
-        return op("p", lambda: g.tensor.matmul(o[0], l[0], x[0], st, sp), [l, x], [o])
+        return op("p", lambda: g.tensor.matmul(o[0], l[0], x[0], st, sp), [l, x], [o], max(64, x[1][0][3]) * PL["pe"] * (4 if wide(x) == 4 else 1))
 
     def iota(o, pat, base=0, cm=0, flt=True):
+        c = 130 + 2 * o[1][0][3] * PL["cyc"]
         if flt:
-            return op("g", lambda: g.iota(o[0], pat, base, cm, allow_small_or_imprecise_dtypes=True), [], [o])
-        return op("g", lambda: g.iota(o[0], pat, base, cm), [], [o])
+            return op("g", lambda: g.iota(o[0], pat, base, cm, allow_small_or_imprecise_dtypes=True), [], [o], c)
+        return op("g", lambda: g.iota(o[0], pat, base, cm), [], [o], c)
 
     def dma(q, sem, o, i):
-        return op(q, lambda: Q[q].dma_start(o[0], i[0]).then_inc(T.sem[sem], 16), [i], [o], sem=sem, inc=16)
+        x = o if o[1] else i
+        return op(q, lambda: Q[q].dma_start(o[0], i[0]).then_inc(T.sem[sem], 16), [i], [o], 128 * x[1][0][3] * wide(x) / PL["bw"], sem=sem, inc=16)
 
     def H(x):
         return (x, [])
@@ -175,14 +199,11 @@ def rank_program(g, core, T, topo):
     rid, pid = topo.addr(nxt)[0:2]
     ne_ = len(topo.engines(core, nxt))
     m_all = topo.mask(core, nxt)
-    sent = [0]
 
     def send(src, dst, rsem, lsem, extra=()):
-        if lsem == "ml":
-            sent[0] += ne_
-        op("g", lambda: g.remote_dma(dst[0], src[0], T.sem[rsem], T.sem[lsem], pid, rid, m_all), [src], [],
-           sem=lsem, inc=sent[0] if lsem == "ml" else ne_, extra=extra)
-        note("rem", (rsem, ne_, {}), [], dst[1])
+        tk = op("g", lambda: g.remote_dma(dst[0], src[0], T.sem[rsem], T.sem[lsem], pid, rid, m_all), [src], [],
+                128 * src[1][0][3] * 2 / PL["bw"], sem=lsem, inc=final.get(lsem, 0) + ne_, extra=extra)
+        note("rem", (rsem, ne_, {}, tk[3]), [], dst[1])
 
     h = O // 2
     dma("a", "ld0", V("pi", 0, 96), H(T.pth[:]))
@@ -199,27 +220,31 @@ def rank_program(g, core, T, topo):
         q = V("qq", 32 * b, 32 * b + 32)
         sh = float(slot(t) - P0 - O)
         L = [lambda: aff(tp(0), q, 1.0, float(-B * S), on),
-             lambda: ts(tp(2), q, float(P0), mx, float(P0 + O - 1), mn),
              lambda: act(tp(8), q, AF.Sign, float(1 - P0)) if on == "a" else ts(tp(8), q, float(P0), ge),
-             lambda: tt(tp(4), tp(2), q, eq),
+             lambda: ts(tp(2), q, float(P0), mx, float(P0 + O - 1), mn),
+             lambda: mm(V("PC", 0, 32), V("blockf", 0, 128), tp(8), True, True),
              lambda: ts(tp(1), tp(0), float(P0 + O), mx, float(P0 + W - 1), mn),
+             lambda: tt(tp(4), tp(2), q, eq),
+             lambda: tt(tp(3), tp(1), tp(0), eq),
              lambda: tt(tp(2), tp(2), tp(4), mul),
-             lambda: (mm(V("PC", 0, 32), V("blockf", 0, 128), tp(8), True, True), tt(tp(3), tp(1), tp(0), eq)),
+             lambda: aff(tp(6), tp(3), float(-O), float(-P0), on),
+             lambda: aff(tp(7), tp(3), sh, 0.0, on),
+             lambda: tt(tp(1), tp(1), tp(3), mul),
              lambda: ts(V("WW", 64 * b + 32, 64 * b + 64), V("PC", 0, 32), C(1), eq),
-             lambda: (aff(tp(6), tp(3), float(-O), float(-P0), on), aff(tp(7), tp(3), sh, 0.0, on), tt(tp(1), tp(1), tp(3), mul)),
              lambda: tt(tp(5), tp(1), tp(2), add),
              lambda: tt(tp(6), tp(6), tp(5), add),
              lambda: tt(tp(7), tp(7), tp(5), add),
              lambda: cp(V("site", 32 * b, 32 * b + 32), tp(6))]
         for jh in range(2):
-            L.append(lambda jh=jh: (cp(V("offL", 32 * b + jh, 32 * b + 32, 2), V("tp", 224 + 16 * jh, 240 + 16 * jh)),
-                                    aff(V("GG", 96 * b + 48 * jh + 32, 96 * b + 48 * jh + 48), V("tp", 160 + 16 * jh, 176 + 16 * jh), 1.0, 0.0, on)))
+            L.append(lambda jh=jh: aff(V("GG", 96 * b + 48 * jh + 32, 96 * b + 48 * jh + 48), V("tp", 160 + 16 * jh, 176 + 16 * jh), 1.0, 0.0, on))
+            L.append(lambda jh=jh: cp(V("offL", 32 * b + jh, 32 * b + 32, 2), V("tp", 224 + 16 * jh, 240 + 16 * jh)))
         return L
 
     iota(V("pint", 0, 1), [[0, 1]], 0, 1, False)
     iota(V("c2", 144, 272), [[1, 8], [0, 16]])
     iota(V("c2", 336, 432), [[32, 3], [1, 16], [16, 2]])
     iota(V("c2", 432, 450), [[16, 6], [0, 3]])
+    iota(V("c2", 450, 464), [[16, 2], [2, 7]])
     iota(V("c2", 0, 144), [[1, 144]])
     iota(V("c2", 272, 320), [[0, 3], [1, 16]])
     iota(V("c2", 320, 326), [[16, 6]], 32)
@@ -238,10 +263,13 @@ def rank_program(g, core, T, topo):
     cp(C(0), V("pint", 0, 1))
     ts(V("pint", 1, 2), V("pint", 0, 1), 15, AluOpType.bitwise_and)
     ts(V("pint", 2, 3), V("pint", 0, 1), 4, AluOpType.arith_shift_right)
+    ts(V("pint", 4, 5), V("pint", 0, 1), 3, AluOpType.arith_shift_right, 1, AluOpType.bitwise_and)
     cp(V("oc", 0, 96), V("c2", 336, 432))
     cp(V("col", 1, 3), V("pint", 1, 3))
+    cp(C(4), V("pint", 4, 5))
     ts(V("c2", 434, 450, 3), V("c2", 434, 450, 3), 96.0, add)
     ts(V("blockf", 0, 128), V("c2", 144, 272), C(2), eq)
+    ts(V("oc", 114, 128), V("c2", 450, 464), C(4), add)
     ts(V("oc", 96, 114), V("c2", 432, 450), C(1), add)
     ts(C(3), C(2), 16.0, mul, 15.0, add)
     ts(C(5), C(1), 16.0, mul)
@@ -262,11 +290,11 @@ def rank_program(g, core, T, topo):
             lambda: ms(V("lowc", 96, 97), 232.0 - WT),
             lambda: ms(V("lowc", 112 + 104, 112 + 105), 232.0 - WT),
             lambda: ts(V("maskT", 0, 48), V("maskT", 0, 48), BIG, mul)]
-    for k, f in enumerate(prep_ops(0, "v")):
+    for f in prep_ops(0, "v") + prep_ops(1, "v"):
+        if more and peek(f)[0] > 40:
+            more.pop(0)()
         f()
-        if k < len(more):
-            more[k]()
-    for f in prep_ops(1, "v"):
+    for f in more:
         f()
     ts(V("detf", 0, h), V("dets", 0, h), float(P0), add)
     ts(V("abf", 0, 512), I(V("dets", 0, O), V("site", 0, 32)), float(P0), add)
@@ -291,11 +319,11 @@ def rank_program(g, core, T, topo):
 
         def spread():
             ts(V("ncd", 16, 32), V("i16", 0, 16), ncol(1), mul)
+            for jh in range(2):
+                mm(V("PC", 32 + 16 * jh, 48 + 16 * jh), V("identf", 0, 128), V("M", 48 * jh + 32, 48 * jh + 48), True, True)
             for ty in range(2):
                 for jh in range(2):
                     mm(V("PB", 32 * ty + 16 * jh, 32 * ty + 16 * jh + 16), blk, V("M", 48 * jh + 16 * ty, 48 * jh + 16 * ty + 16), True, True)
-            for jh in range(2):
-                mm(V("PC", 32 + 16 * jh, 48 + 16 * jh), V("identf", 0, 128), V("M", 48 * jh + 32, 48 * jh + 48), True, True)
             for k in range(2):
                 mm(V("PB", 64 + 32 * k, 96 + 32 * k), blk, V("ncd", 0, 32), True, True)
             act(V("WW", 64 * b, 64 * b + 32), V("PC", 32, 64), AF.Sign)
@@ -349,12 +377,12 @@ def rank_program(g, core, T, topo):
              lambda: scan(V("XO", 48 * jh, 48 * jh + 48), V("cscan", 0, 48), V(bank, c0, c0 + 48), 0.0, mul, mx),
              lambda: ts(mk, x, P0 + O + BIG, ge, sh, mul),
              cmp_(0),
-             lambda: tt(y, x, mk, add),
              cmp_(1),
-             lambda: ts(oD, y, -BIG, add),
+             lambda: tt(y, x, mk, add),
              cmp_(2),
-             lambda: tt(nD, I(V("D", 0, slot(t) + S), oD), V("delta", g0, g0 + 48), add),
-             lambda: scan(V("ns", 144 * jh, 144 * jh + hw), V("ne", 0, hw), V("ne", hw, 2 * hw), 1.0, mn, mn)]
+             lambda: ts(oD, y, -BIG, add),
+             lambda: scan(V("ns", 144 * jh, 144 * jh + hw), V("ne", 0, hw), V("ne", hw, 2 * hw), 1.0, mn, mn),
+             lambda: tt(nD, I(V("D", 0, slot(t) + S), oD), V("delta", g0, g0 + 48), add)]
         own = []
         for c in range(3):
             k = 3 * jh + c
@@ -363,11 +391,11 @@ def rank_program(g, core, T, topo):
         if t == ST - 1:
             return L + own + [lambda: cp(I(V("D", 0, slot(t) + S), V("oo", 4 * jh, 4 * jh + 3)), nD)], []
         L.insert(14, lambda: ts(ym, y, -BIG - sh, add))
-        L.append(lambda: ts(V("mo", m0 + 8, m0 + 56), nD, -1.0, mul))
-        L.append(lambda: ts(V("mo", m0 + 56, m0 + 104), nD, 256.0, add))
         for c in range(3):
             k = 3 * jh + c
             L.append(lambda c=c, k=k: ts(V("mo", m0 + c, m0 + c + 1), V("yy", y0 + 8 + c, y0 + 9 + c), nc, mul, V("tr", k, k + 1), mx))
+        L.append(lambda: ts(V("mo", m0 + 8, m0 + 56), nD, -1.0, mul))
+        L.append(lambda: ts(V("mo", m0 + 56, m0 + 104), nD, 256.0, add))
         L.append(lambda: send(V("mo", m0, m0 + MS), V("lo", m0, m0 + MS), "ma%d" % (2 * t + jh), "ml"))
         return L, own
 
@@ -386,21 +414,40 @@ def rank_program(g, core, T, topo):
         b = t % 3
         act(V("abf", 512 * b, 512 * b + 512), I(V("detf", 0, O), V("site", 32 * b, 32 * b + 32)), AF.Copy)
 
-    def narrow(t, k):
-        c = 512 * (t % 3) + 256 * k
-        cp(V("ab16", c, c + 256), V("abf", c, c + 256))
+    def narrow(t):
+        c0 = 512 * (t % 3)
+        return [lambda c=c: cp(V("ab16", c, c + 128), V("abf", c, c + 128)) for c in range(c0, c0 + 512, 128)]
+
+    def fill(gap, lists):
+        for l in lists:
+            while l and peek(l[0])[2] != "v":
+                l.pop(0)()
+            if l:
+                w, c, q = peek(l[0])
+                if w + c <= gap + 40:
+                    l.pop(0)()
+                    return True
+        return False
+
+    def chain(fs, lists):
+        for f in fs:
+            while peek(f)[2] == "v" and peek(f)[0] > 30 and fill(peek(f)[0], lists):
+                pass
+            f()
 
     spill = prep_ops(2)
+    head = []
     bulk(0)
     for t in range(ST):
         b = t % 3
         R = 12 if t < 3 else 13
-        left = [41, 41]
+        nl = 8 if PL["strided"] else 1
+        left = [33 + nl, 33 + nl]
         lowv = V("lowc", 0 if R == 12 else 112, 112 if R == 12 else 224)
 
         def smm(jh, n, l, x, k=0, st=1):
             left[jh] -= 1
-            mm(V("S%d" % jh, k, n, st), l, x, left[jh] == 40, left[jh] == 0)
+            mm(V("S%d" % jh, k, n, st), l, x, left[jh] == 32 + nl, left[jh] == 0)
 
         def flow(j, q):
             jh, j16 = divmod(j, 16)
@@ -424,88 +471,75 @@ def rank_program(g, core, T, topo):
             for j16 in range(16):
                 mm(V("PL", 0, 32), V("Zn", 15 - j16, 143 - j16), V("XL", 32 * j16, 32 * j16 + 32), j16 == 0, j16 == 15)
 
-        def lexp():
+        def lcopy():
             act(V("Lsb", 0, 32), V("PL", 0, 32), AF.Copy)
             for jh in range(2):
-                for k in range(8):
+                for k in range(8 if PL["strided"] else 0):
                     smm(jh, 8 * R, V("identb", 0, 128), V("Lsb", 16 * jh, 16 * jh + R), k, 8)
 
-        fc = 16 * R * 1.5
-        a0, a1 = NA0[t], NA1[t]
+        def lexp():
+            act(V("Lexp", 0, 224), I(V("Lsb", 0, 32), V("oc", 114, 128)), AF.Copy)
+            for jh in range(2):
+                smm(jh, 112, V("identb", 0, 128), V("Lexp", 112 * jh, 112 * jh + 112))
+
+        fv_ = 50 + 16 * R * PL["gat"] * PL["cyc"]
         t0, t0b = tail_ops(t, 0)
         t1, t1b = tail_ops(t, 1)
-        A = [(80 + fc, None, "f0", lambda j=j: flow(j, "a")) for j in range(a0)]
-        A[LP:LP] = [(100, "lr", "f0", lexp)]
-        A += [(80 + fc, None, "f1", lambda j=j: flow(j, "a")) for j in range(16, 16 + a1)]
-        fl0 = [(60 + fc, None, "f0", lambda j=j: flow(j, "v")) for j in range(a0, 16)]
-        fl1 = [(60 + fc, None, "f1", lambda j=j: flow(j, "v")) for j in range(16 + a1, 32)]
-        Vq = [(830, None, None, lambda: tt(V("XL", 0, 512), I(V("D", 0, slot(t) + S), V("offL", 32 * b, 32 * b + 32)),
-                                           V("fexp", 512 * b, 512 * b + 512), mn)),
-              fl0.pop(), (260, None, "lr", lrelu)] + fl0
-        small = [(70, None, None, f) for f in spill]
-        for z in range(PRE):
-            Vq.append(fl1.pop())
-        for k, f in enumerate(t0):
-            Vq.append((80, "f0" if k == 0 else None, None, f))
-            if fl1 and (k == 6 or k in FL):
-                Vq.append(fl1.pop())
-            elif k < 9 and small:
-                n = -(-len(small) // (9 - k))
-                Vq += small[:n]
-                small = small[n:]
-        Vq += small + fl1
-        need = {"f0": 17, "lr": 1}
-        tm = {"a": 0.0, "v": 300.0}
-        while A or Vq:
-            q = sorted([q for q, l in (("a", A), ("v", Vq)) if l and need.get(l[0][1], 0) == 0],
-                       key=lambda q: tm[q] + (A if q == "a" else Vq)[0][0])[0]
-            it = (A if q == "a" else Vq).pop(0)
-            it[3]()
-            tm[q] += it[0]
-            if it[2] in need:
-                need[it[2]] -= 1
+        Lv = head + [lambda: tt(V("XL", 0, 512), I(V("D", 0, slot(t) + S), V("offL", 32 * b, 32 * b + 32)), V("fexp", 512 * b, 512 * b + 512), mn), lrelu]
+        La = [lcopy] + ([] if PL["strided"] else [lexp])
+        flows = list(range(32))
+        while flows or Lv or La or t0:
+            a_on = flows or (La and not Lv)
+            if a_on and clock["a"] <= clock["v"]:
+                if La and not Lv and (not flows or peek(La[0])[0] < 40):
+                    La.pop(0)()
+                else:
+                    flow(flows.pop(0), "a")
+                continue
+            ch = Lv or (t0 if left[0] == 0 else [])
+            gap = peek(ch[0])[0] if ch else 1e9
+            if ch and (gap < 40 or peek(ch[0])[2] != "v"):
+                ch.pop(0)()
+                continue
+            take_flow = flows and (flows[0] < 16 or clock["v"] + fv_ + 75 * len(t0) <= clock["a"] + (fv_ + 15) * len(flows))
+            if take_flow and gap > 0.45 * fv_:
+                flow(flows.pop(0), "v")
+            elif fill(min(gap, 200), [spill]):
+                pass
+            elif take_flow and gap > 60:
+                flow(flows.pop(0), "v")
+            elif ch:
+                ch.pop(0)()
+            elif a_on:
+                clock["v"] = clock["a"] + 1
         p1, p2 = path_ops(t)
         if t == ST - 1:
-            p1[0]()
-            for f in t1:
-                f()
+            chain(t1, [p1[0:1], spill])
             dma("s", "st0", H(T.yd[:, 0:O]), V("D", P0, P0 + O))
             dma("a", "st1", H(T.yd[:, O:W]), V("D", slot(t), slot(t) + S))
-            for f in p1[1:] + p2:
+            for f in spill + p1 + p2:
                 f()
             dma("s", "st2", H(T.yp[:]), V("ypo", 0, 96))
             break
         act(V("NN", P0 + O, P0 + W), V("D", slot(t + 1), slot(t + 1) + S), AF.Relu, None, -1.0)
         if t == 0:
             detours(1)
-        else:
-            narrow(t + 1, 0)
         k0, k1 = take(t, 0), take(t, 1)
-        gaps = t0b + [p1[0]]
-        for k, f in enumerate(t1):
-            f()
-            if k == 6 and t > 0:
-                narrow(t + 1, 1)
-            elif gaps and (k in GAPS or k == 6):
-                gaps.pop(0)()
+        g1, g2 = t0b + p1[0:1], narrow(t + 1)
+        chain(t1, [g2, g1, spill] if t else [g1, spill])
         act(V("nn", 0, 96), V("nd", 0, 96), AF.Relu, None, -1.0)
-        for f in gaps + t1b + p1[1:] + k0[1:2]:
+        for f in g1 + t1b + p1[1:] + k0[1:2]:
             f()
+        must = [lambda: cp(I(V("D", 0, slot(t) + S), V("oo", 0, 6)), V("nd", 0, 96)),
+                lambda: cp(I(V("NN", 0, slot(t) + S), V("oo", 0, 6)), V("nn", 0, 96)), k0[2], k0[0]]
+        chain(must, [spill, g2, p2])
+        chain(spill + g2, [p2])
         if t + 2 < ST:
             detours(t + 2)
-        cp(I(V("D", 0, slot(t) + S), V("oo", 0, 6)), V("nd", 0, 96))
-        if t == 0:
-            narrow(1, 0)
-            narrow(1, 1)
-        cp(I(V("NN", 0, slot(t) + S), V("oo", 0, 6)), V("nn", 0, 96))
-        k0[2]()
-        k0[0]()
-        later = p2 + (prep_ops(t + 3) if t + 3 < ST else [])
-        for f in later[:KEEP[t]]:
-            f()
-        spill = later[KEEP[t]:]
-        for f in k1:
-            f()
-        bulk(t + 1)
+        spill = p2 + (prep_ops(t + 3) if t + 3 < ST else [])
+        while spill and fill(peek(k1[0])[0] - 100, [spill]):
+            pass
+        k1[0]()
+        head = [k1[1], lambda t=t, f=k1[2]: (f(), bulk(t + 1))]
     for sem, v in final.items():
         g.sync.wait_ge(T.sem[sem], v)

@@ -8,7 +8,7 @@ DW = SB + ST * S
 BIG = 8192.0
 WT = 1024.0
 XS = 208
-MS = 104
+MS = 56
 
 SCRATCH = {
     "D": ("sbuf", [128, DW], "bfloat16"), "NN": ("sbuf", [128, DW], "float32"),
@@ -24,14 +24,14 @@ SCRATCH = {
     "col": ("sbuf", [128, 16], "float32"),
     "identf": ("sbuf", [128, 128], "float32"), "identb": ("sbuf", [128, 128], "bfloat16"), "blockf": ("sbuf", [128, 128], "float32"),
     "Zp": ("sbuf", [128, 144], "bfloat16"), "Zn": ("sbuf", [128, 144], "bfloat16"),
-    "maskT": ("sbuf", [128, 48], "float32"), "cscan": ("sbuf", [128, 48], "float32"), "i16": ("sbuf", [128, 48], "float32"),
+    "maskT": ("sbuf", [128, 48], "bfloat16"), "cscan": ("sbuf", [128, 48], "float32"), "i16": ("sbuf", [128, 48], "float32"),
     "MW": ("sbuf", [128, 768], "float32"), "lowc": ("sbuf", [128, 224], "bfloat16"),
     "oc": ("sbuf", [128, 144], "uint16"), "tr": ("sbuf", [128, 8], "bfloat16"), "c4": ("sbuf", [128, 4], "float32"),
-    "Lsb": ("sbuf", [128, 32], "bfloat16"), "Lexp": ("sbuf", [128, 224], "bfloat16"),
+    "Lsb": ("sbuf", [128, 32], "bfloat16"),
     "key": ("sbuf", [128, 8], "float32"), "u": ("sbuf", [128, 16], "int32"), "o16": ("sbuf", [128, 32], "uint16"),
     "M": ("sbuf", [128, 96], "float32"), "XO": ("sbuf", [128, 96], "float32"), "ne": ("sbuf", [128, 288], "bfloat16"),
-    "ns": ("sbuf", [128, 288], "bfloat16"), "nd": ("sbuf", [128, 96], "float32"), "nn": ("sbuf", [128, 96], "float32"),
-    "rd": ("sbuf", [128, 96], "float32"),
+    "ns": ("sbuf", [128, 288], "bfloat16"), "nd": ("sbuf", [128, 576], "bfloat16"), "nn": ("sbuf", [128, 96], "float32"),
+    "ndf": ("sbuf", [128, 576], "float32"), "rd": ("sbuf", [128, 480], "float32"),
     "yy": ("sbuf", [128, 32], "float32"), "ncd": ("sbuf", [128, 32], "float32"), "oo": ("sbuf", [128, 8], "uint16"),
     "mo": ("sbuf", [128, 10 * MS], "uint16"), "lo": ("sbuf", [128, 10 * MS], "uint16"),
     "S0": ("psum", [128, 512], "float32"), "S1": ("psum", [128, 512], "float32"), "PL": ("psum", [128, 512], "float32"),
@@ -39,10 +39,11 @@ SCRATCH = {
     "PC": ("psum", [128, 512], "float32"),
 }
 PSUM = ("S0", "S1", "PL", "NA", "NB", "PB", "PC")
-SEMAPHORES = (["qv", "qa", "qp", "qg", "ml"] + ["ld%d" % k for k in range(7)] + ["st%d" % k for k in range(3)]
-              + ["ba%d" % k for k in range(5)] + ["ma%d" % k for k in range(10)] + ["bl%d" % k for k in range(5)])
+SEMAPHORES = (["qv", "qa", "qp", "qg", "ml"] + ["ld%d" % k for k in range(8)] + ["st%d" % k for k in range(3)]
+              + ["ba%d" % k for k in range(5)] + ["ma%d" % k for k in range(10)] + ["md%d" % k for k in range(10)]
+              + ["bl%d" % k for k in range(5)])
 
-PL = {"cyc": 0.9, "gat": 1.4, "sca": 3.5, "pe": 0.6, "lat": 120.0, "rem": 2000.0, "bw": 250.0, "strided": False}
+PL = {"cyc": 0.9, "gat": 1.4, "sca": 3.5, "pe": 0.6, "lat": 120.0, "rem": 2000.0, "bw": 250.0, "cut": 14}
 add, sub, mul, mx, mn = AluOpType.add, AluOpType.subtract, AluOpType.mult, AluOpType.max, AluOpType.min
 eq, neq, ge, gt = AluOpType.is_equal, AluOpType.not_equal, AluOpType.is_ge, AluOpType.is_gt
 AF = ActivationFunctionType
@@ -205,14 +206,15 @@ def rank_program(g, core, T, topo):
                 128 * src[1][0][3] * 2 / PL["bw"], sem=lsem, inc=final.get(lsem, 0) + ne_, extra=extra)
         note("rem", (rsem, ne_, {}, tk[3]), [], dst[1])
 
-    h = O // 2
+    h, h2 = O // 2, 2304
     dma("a", "ld0", V("pi", 0, 96), H(T.pth[:]))
     dma("s", "ld1", V("ff", 0, 96), H(T.fv[:]))
     dma("s", "ld2", V("dets", 0, h), H(T.det[:, 0:h]))
     dma("s", "ld6", V("dets", h, O), H(T.det[:, h:O]))
     dma("s", "ld3", V("D", SB, SB + S), H(T.dn[:, O:W]))
     dma("s", "ld4", V("D", P0, P0 + h), H(T.dn[:, 0:h]))
-    last_load = dma("s", "ld5", V("D", P0 + h, P0 + O), H(T.dn[:, h:O]))
+    dma("s", "ld5", V("D", P0 + h, P0 + h2), H(T.dn[:, h:h2]))
+    last_load = dma("s", "ld7", V("D", P0 + h2, P0 + O), H(T.dn[:, h2:O]))
 
     def prep_ops(t, on="a"):
         b = t % 3
@@ -244,7 +246,6 @@ def rank_program(g, core, T, topo):
     iota(V("c2", 144, 272), [[1, 8], [0, 16]])
     iota(V("c2", 336, 432), [[32, 3], [1, 16], [16, 2]])
     iota(V("c2", 432, 450), [[16, 6], [0, 3]])
-    iota(V("c2", 450, 464), [[16, 2], [2, 7]])
     iota(V("c2", 0, 144), [[1, 144]])
     iota(V("c2", 272, 320), [[0, 3], [1, 16]])
     iota(V("c2", 320, 326), [[16, 6]], 32)
@@ -263,13 +264,10 @@ def rank_program(g, core, T, topo):
     cp(C(0), V("pint", 0, 1))
     ts(V("pint", 1, 2), V("pint", 0, 1), 15, AluOpType.bitwise_and)
     ts(V("pint", 2, 3), V("pint", 0, 1), 4, AluOpType.arith_shift_right)
-    ts(V("pint", 4, 5), V("pint", 0, 1), 3, AluOpType.arith_shift_right, 1, AluOpType.bitwise_and)
     cp(V("oc", 0, 96), V("c2", 336, 432))
     cp(V("col", 1, 3), V("pint", 1, 3))
-    cp(C(4), V("pint", 4, 5))
     ts(V("c2", 434, 450, 3), V("c2", 434, 450, 3), 96.0, add)
     ts(V("blockf", 0, 128), V("c2", 144, 272), C(2), eq)
-    ts(V("oc", 114, 128), V("c2", 450, 464), C(4), add)
     ts(V("oc", 96, 114), V("c2", 432, 450), C(1), add)
     ts(C(3), C(2), 16.0, mul, 15.0, add)
     ts(C(5), C(1), 16.0, mul)
@@ -283,28 +281,29 @@ def rank_program(g, core, T, topo):
     act(V("fexp", 0, 1536), I(V("ff", 0, 96), V("oc", 0, 96)), AF.Copy)
     act(V("delta", 0, 288), I(V("ff", 0, 192), V("oc", 96, 114)), AF.Copy)
     more = [lambda: ts(V("i16", 0, 48), V("c2", 272, 320), C(1), eq),
-            lambda: ts(V("maskT", 0, 48), V("c2", 272, 320), C(1), gt),
+            lambda: ts(V("nn", 0, 48), V("c2", 272, 320), C(1), gt),
             lambda: ts(V("cscan", 0, 48), V("c2", 272, 320), C(1), neq),
             lambda: ts(V("tr", 0, 6), V("c2", 320, 326), C(1), add),
-            lambda: tt(V("maskT", 0, 48), V("i16", 0, 48), V("maskT", 0, 48), sub),
+            lambda: tt(V("nn", 0, 48), V("i16", 0, 48), V("nn", 0, 48), sub),
             lambda: ms(V("lowc", 96, 97), 232.0 - WT),
             lambda: ms(V("lowc", 112 + 104, 112 + 105), 232.0 - WT),
-            lambda: ts(V("maskT", 0, 48), V("maskT", 0, 48), BIG, mul)]
-    for f in prep_ops(0, "v") + prep_ops(1, "v"):
+            lambda: ts(V("maskT", 0, 48), V("nn", 0, 48), BIG, mul)]
+    for f in prep_ops(0, "v") + prep_ops(1, "v") + prep_ops(2, "v"):
         if more and peek(f)[0] > 40:
             more.pop(0)()
         f()
     for f in more:
         f()
+    ts(V("MW", 0, 768), V("ci", 0, 768), C(1), eq)
     ts(V("detf", 0, h), V("dets", 0, h), float(P0), add)
     ts(V("abf", 0, 512), I(V("dets", 0, O), V("site", 0, 32)), float(P0), add)
-    ts(V("MW", 0, 768), V("ci", 0, 768), C(1), eq)
-    cp(V("ab16", 0, 512), V("abf", 0, 512))
     ts(V("detf", h, O), V("dets", h, O), float(P0), add)
+    cp(V("ab16", 0, 512), V("abf", 0, 512))
     act(V("NN", P0 + O, P0 + W), V("D", SB, SB + S), AF.Relu, None, -1.0)
     act(V("NN", P0, P0 + h), V("D", P0, P0 + h), AF.Relu, None, -1.0)
-    hh = P0 + h + 640
-    act(V("NN", P0 + h, hh), V("D", P0 + h, hh), AF.Relu, None, -1.0)
+    ts(V("NN", P0 + h, P0 + h2), V("D", P0 + h, P0 + h2), -1.0, mul, 0.0, mx)
+    hh = P0 + h2 + 256
+    act(V("NN", P0 + h2, hh), V("D", P0 + h2, hh), AF.Relu, None, -1.0)
     ts(V("NN", hh, P0 + O), V("D", hh, P0 + O), -1.0, mul, 0.0, mx)
 
     def ncol(jh):
@@ -353,7 +352,8 @@ def rank_program(g, core, T, topo):
         x = V("XO", 48 * jh + 15, 48 * jh + 48, 16)
         y0 = 16 * jh
         mk, y, ym = V("yy", y0, y0 + 3), V("yy", y0 + 4, y0 + 7), V("yy", y0 + 8, y0 + 11)
-        nD = V("nd", 48 * jh, 48 * jh + 48)
+        n0 = 96 * t + 48 * jh
+        nD = V("ndf", n0, n0 + 48)
         m0 = MS * (2 * t + jh)
         hw = 3 * wd // 2
 
@@ -362,7 +362,7 @@ def rank_program(g, core, T, topo):
             mm(V(bank, c0, c0 + 48), V("blockf", 0, 128), Mv, False, True)
             if jh == 0:
                 mm(V("NB", 0, 48), V("blockf", 0, 128), Mv, True, True)
-                mm(V("NB", 48, 96), V("identf", 0, 128), V("maskT", 0, 48), True, False)
+                mm(V("NB", 48, 96), V("identb", 0, 128), V("maskT", 0, 48), True, False)
 
         def cmp_(c):
             xc = V("XO", 48 * jh + 16 * c + 15, 48 * jh + 16 * c + 16)
@@ -395,16 +395,16 @@ def rank_program(g, core, T, topo):
             k = 3 * jh + c
             L.append(lambda c=c, k=k: ts(V("mo", m0 + c, m0 + c + 1), V("yy", y0 + 8 + c, y0 + 9 + c), nc, mul, V("tr", k, k + 1), mx))
         L.append(lambda: ts(V("mo", m0 + 8, m0 + 56), nD, -1.0, mul))
-        L.append(lambda: ts(V("mo", m0 + 56, m0 + 104), nD, 256.0, add))
-        L.append(lambda: send(V("mo", m0, m0 + MS), V("lo", m0, m0 + MS), "ma%d" % (2 * t + jh), "ml"))
+        L.append(lambda: (send(V("mo", m0, m0 + MS), V("lo", m0, m0 + MS), "ma%d" % (2 * t + jh), "ml"),
+                          send(nD, V("rd", n0, n0 + 48), "md%d" % (2 * t + jh), "ml")))
         return L, own
 
     def take(t, jh):
         m0 = MS * (2 * t + jh)
+        n0 = 96 * t + 48 * jh
         off = V("lo", m0, m0 + 3)
         return [lambda: cp(I(V("NN", 0, P0 + W), off), V("lo", m0 + 8, m0 + 56)),
-                lambda: ts(V("rd", 48 * jh, 48 * jh + 48), V("lo", m0 + 56, m0 + 104), -256.0, add),
-                lambda: cp(I(V("D", slot(t + 1) - P0 - O, slot(t + 1) + S), off), V("rd", 48 * jh, 48 * jh + 48))]
+                lambda: cp(I(V("D", slot(t + 1) - P0 - O, slot(t + 1) + S), off), V("rd", n0, n0 + 48))]
 
     def bulk(t):
         if t < ST - 1:
@@ -435,19 +435,18 @@ def rank_program(g, core, T, topo):
                 pass
             f()
 
-    spill = prep_ops(2)
+    spill = []
     head = []
     bulk(0)
     for t in range(ST):
         b = t % 3
         R = 12 if t < 3 else 13
-        nl = 8 if PL["strided"] else 1
-        left = [33 + nl, 33 + nl]
+        left = [41, 41]
         lowv = V("lowc", 0 if R == 12 else 112, 112 if R == 12 else 224)
 
         def smm(jh, n, l, x, k=0, st=1):
             left[jh] -= 1
-            mm(V("S%d" % jh, k, n, st), l, x, left[jh] == 32 + nl, left[jh] == 0)
+            mm(V("S%d" % jh, k, n, st), l, x, left[jh] == 40, left[jh] == 0)
 
         def flow(j, q):
             jh, j16 = divmod(j, 16)
@@ -464,7 +463,7 @@ def rank_program(g, core, T, topo):
 
         for jh in range(2):
             smm(jh, 112, V("identb", 0, 128), lowv)
-        mm(V("NA", 0, 48), V("identf", 0, 128), V("maskT", 0, 48), True, False)
+        mm(V("NA", 0, 48), V("identb", 0, 128), V("maskT", 0, 48), True, False)
 
         def lrelu():
             ts(V("XL", 0, 512), V("XL", 0, 512), 0.0, mx)
@@ -474,19 +473,16 @@ def rank_program(g, core, T, topo):
         def lcopy():
             act(V("Lsb", 0, 32), V("PL", 0, 32), AF.Copy)
             for jh in range(2):
-                for k in range(8 if PL["strided"] else 0):
+                for k in range(8):
                     smm(jh, 8 * R, V("identb", 0, 128), V("Lsb", 16 * jh, 16 * jh + R), k, 8)
-
-        def lexp():
-            act(V("Lexp", 0, 224), I(V("Lsb", 0, 32), V("oc", 114, 128)), AF.Copy)
-            for jh in range(2):
-                smm(jh, 112, V("identb", 0, 128), V("Lexp", 112 * jh, 112 * jh + 112))
 
         fv_ = 50 + 16 * R * PL["gat"] * PL["cyc"]
         t0, t0b = tail_ops(t, 0)
         t1, t1b = tail_ops(t, 1)
+        t0x = t0[PL["cut"]:]
+        t0 = t0[:PL["cut"]]
         Lv = head + [lambda: tt(V("XL", 0, 512), I(V("D", 0, slot(t) + S), V("offL", 32 * b, 32 * b + 32)), V("fexp", 512 * b, 512 * b + 512), mn), lrelu]
-        La = [lcopy] + ([] if PL["strided"] else [lexp])
+        La = [lcopy]
         flows = list(range(32))
         while flows or Lv or La or t0:
             a_on = flows or (La and not Lv)
@@ -514,10 +510,13 @@ def rank_program(g, core, T, topo):
                 clock["v"] = clock["a"] + 1
         p1, p2 = path_ops(t)
         if t == ST - 1:
-            chain(t1, [p1[0:1], spill])
+            chain(t1[:8], [t0x, spill])
+            chain(t0x[:], [])
+            p1[0]()
+            chain(t1[8:], [spill])
             dma("s", "st0", H(T.yd[:, 0:O]), V("D", P0, P0 + O))
             dma("a", "st1", H(T.yd[:, O:W]), V("D", slot(t), slot(t) + S))
-            for f in spill + p1 + p2:
+            for f in spill + p1[1:] + p2:
                 f()
             dma("s", "st2", H(T.yp[:]), V("ypo", 0, 96))
             break
@@ -526,12 +525,15 @@ def rank_program(g, core, T, topo):
             detours(1)
         k0, k1 = take(t, 0), take(t, 1)
         g1, g2 = t0b + p1[0:1], narrow(t + 1)
-        chain(t1, [g2, g1, spill] if t else [g1, spill])
-        act(V("nn", 0, 96), V("nd", 0, 96), AF.Relu, None, -1.0)
-        for f in g1 + t1b + p1[1:] + k0[1:2]:
+        chain(t1[:9], [t0x, g2, spill] if t else [t0x, spill])
+        chain(t0x[:], [])
+        chain(t1[9:], [g2, g1, spill] if t else [g1, spill])
+        nD = V("ndf", 96 * t, 96 * t + 96)
+        act(V("nn", 0, 96), nD, AF.Relu, None, -1.0)
+        for f in g1 + t1b + p1[1:]:
             f()
-        must = [lambda: cp(I(V("D", 0, slot(t) + S), V("oo", 0, 6)), V("nd", 0, 96)),
-                lambda: cp(I(V("NN", 0, slot(t) + S), V("oo", 0, 6)), V("nn", 0, 96)), k0[2], k0[0]]
+        must = [lambda: cp(I(V("D", 0, slot(t) + S), V("oo", 0, 6)), nD),
+                lambda: cp(I(V("NN", 0, slot(t) + S), V("oo", 0, 6)), V("nn", 0, 96)), k0[1], k0[0]]
         chain(must, [spill, g2, p2])
         chain(spill + g2, [p2])
         if t + 2 < ST:
@@ -540,6 +542,6 @@ def rank_program(g, core, T, topo):
         while spill and fill(peek(k1[0])[0] - 100, [spill]):
             pass
         k1[0]()
-        head = [k1[1], lambda t=t, f=k1[2]: (f(), bulk(t + 1))]
+        head = [lambda t=t, f=k1[1]: (f(), bulk(t + 1))]
     for sem, v in final.items():
         g.sync.wait_ge(T.sem[sem], v)

@@ -19,7 +19,7 @@ SCRATCH = {
     "fexp": ("sbuf", [128, 1536], "bfloat16"), "delta": ("sbuf", [128, 288], "bfloat16"),
     "abf": ("sbuf", [128, 1536], "float32"), "ab16": ("sbuf", [128, 1536], "uint16"),
     "GG": ("sbuf", [128, 288], "float32"), "offL": ("sbuf", [128, 96], "uint16"), "site": ("sbuf", [128, 96], "uint16"),
-    "WW": ("sbuf", [128, 192], "float32"), "tp": ("sbuf", [128, 512], "float32"),
+    "WW": ("sbuf", [128, 192], "float32"), "tp": ("sbuf", [128, 1088], "float32"),
     "ci": ("sbuf", [128, 768], "float32"), "c2": ("sbuf", [128, 464], "float32"), "pint": ("sbuf", [128, 8], "int32"),
     "col": ("sbuf", [128, 16], "float32"),
     "identf": ("sbuf", [128, 128], "float32"), "identb": ("sbuf", [128, 128], "bfloat16"), "blockf": ("sbuf", [128, 128], "float32"),
@@ -30,7 +30,7 @@ SCRATCH = {
     "Lsb": ("sbuf", [128, 32], "bfloat16"),
     "key": ("sbuf", [128, 8], "float32"), "u": ("sbuf", [128, 16], "int32"), "o16": ("sbuf", [128, 32], "uint16"),
     "M": ("sbuf", [128, 96], "float32"), "XO": ("sbuf", [128, 96], "float32"), "ne": ("sbuf", [128, 288], "bfloat16"),
-    "ns": ("sbuf", [128, 288], "bfloat16"), "nd": ("sbuf", [128, 576], "bfloat16"), "nn": ("sbuf", [128, 96], "float32"),
+    "ns": ("sbuf", [128, 288], "bfloat16"), "nn": ("sbuf", [128, 96], "float32"),
     "ndf": ("sbuf", [128, 576], "float32"), "rd": ("sbuf", [128, 480], "float32"),
     "yy": ("sbuf", [128, 32], "float32"), "ncd": ("sbuf", [128, 32], "float32"), "oo": ("sbuf", [128, 8], "uint16"),
     "mo": ("sbuf", [128, 10 * MS], "uint16"), "lo": ("sbuf", [128, 10 * MS], "uint16"),
@@ -43,7 +43,7 @@ SEMAPHORES = (["qv", "qa", "qp", "qg", "ml"] + ["ld%d" % k for k in range(8)] + 
               + ["ba%d" % k for k in range(5)] + ["ma%d" % k for k in range(10)] + ["md%d" % k for k in range(10)]
               + ["bl%d" % k for k in range(5)])
 
-PL = {"cyc": 0.9, "gat": 1.4, "sca": 3.5, "pe": 0.6, "lat": 120.0, "rem": 2000.0, "bw": 250.0, "cut": 14}
+PL = {"cyc": 0.9, "gat": 1.4, "sca": 3.5, "pe": 0.45, "lat": 140.0, "rem": 2000.0, "bw": 250.0, "cut": 11}
 add, sub, mul, mx, mn = AluOpType.add, AluOpType.subtract, AluOpType.mult, AluOpType.max, AluOpType.min
 eq, neq, ge, gt = AluOpType.is_equal, AluOpType.not_equal, AluOpType.is_ge, AluOpType.is_gt
 AF = ActivationFunctionType
@@ -193,7 +193,7 @@ def rank_program(g, core, T, topo):
     def C(k):
         return V("col", k, k + 1)
 
-    def tp(k, n=1):
+    def tq(k, n=1):
         return V("tp", 32 * k, 32 * (k + n))
 
     nxt = T.cores[(r - 1) % NR]
@@ -209,22 +209,26 @@ def rank_program(g, core, T, topo):
     h, h2 = O // 2, 2304
     dma("a", "ld0", V("pi", 0, 96), H(T.pth[:]))
     dma("s", "ld1", V("ff", 0, 96), H(T.fv[:]))
-    dma("s", "ld2", V("dets", 0, h), H(T.det[:, 0:h]))
-    dma("s", "ld6", V("dets", h, O), H(T.det[:, h:O]))
+    dma("s", "ld2", V("dets", 0, O), H(T.det[:]))
     dma("s", "ld3", V("D", SB, SB + S), H(T.dn[:, O:W]))
     dma("s", "ld4", V("D", P0, P0 + h), H(T.dn[:, 0:h]))
     dma("s", "ld5", V("D", P0 + h, P0 + h2), H(T.dn[:, h:h2]))
     last_load = dma("s", "ld7", V("D", P0 + h2, P0 + O), H(T.dn[:, h2:O]))
 
-    def prep_ops(t, on="a"):
+    def prep_ops(t, on="a", z=0):
         b = t % 3
         B = (r + t) % NR
         q = V("qq", 32 * b, 32 * b + 32)
         sh = float(slot(t) - P0 - O)
+        k0 = (0, 14, 24)[z]
+        pc = V("PC", (0, 64, 96)[z], (0, 64, 96)[z] + 32)
+
+        def tp(k):
+            return tq(k0 + k)
         L = [lambda: aff(tp(0), q, 1.0, float(-B * S), on),
              lambda: act(tp(8), q, AF.Sign, float(1 - P0)) if on == "a" else ts(tp(8), q, float(P0), ge),
              lambda: ts(tp(2), q, float(P0), mx, float(P0 + O - 1), mn),
-             lambda: mm(V("PC", 0, 32), V("blockf", 0, 128), tp(8), True, True),
+             lambda: mm(pc, V("blockf", 0, 128), tp(8), True, True),
              lambda: ts(tp(1), tp(0), float(P0 + O), mx, float(P0 + W - 1), mn),
              lambda: tt(tp(4), tp(2), q, eq),
              lambda: tt(tp(3), tp(1), tp(0), eq),
@@ -232,14 +236,15 @@ def rank_program(g, core, T, topo):
              lambda: aff(tp(6), tp(3), float(-O), float(-P0), on),
              lambda: aff(tp(7), tp(3), sh, 0.0, on),
              lambda: tt(tp(1), tp(1), tp(3), mul),
-             lambda: ts(V("WW", 64 * b + 32, 64 * b + 64), V("PC", 0, 32), C(1), eq),
+             lambda: ts(V("WW", 64 * b + 32, 64 * b + 64), pc, C(1), eq),
              lambda: tt(tp(5), tp(1), tp(2), add),
              lambda: tt(tp(6), tp(6), tp(5), add),
              lambda: tt(tp(7), tp(7), tp(5), add),
              lambda: cp(V("site", 32 * b, 32 * b + 32), tp(6))]
         for jh in range(2):
-            L.append(lambda jh=jh: aff(V("GG", 96 * b + 48 * jh + 32, 96 * b + 48 * jh + 48), V("tp", 160 + 16 * jh, 176 + 16 * jh), 1.0, 0.0, on))
-            L.append(lambda jh=jh: cp(V("offL", 32 * b + jh, 32 * b + 32, 2), V("tp", 224 + 16 * jh, 240 + 16 * jh)))
+            c5, c7 = 32 * (k0 + 5) + 16 * jh, 32 * (k0 + 7) + 16 * jh
+            L.append(lambda jh=jh, c5=c5: aff(V("GG", 96 * b + 48 * jh + 32, 96 * b + 48 * jh + 48), V("tp", c5, c5 + 16), 1.0, 0.0, "a"))
+            L.append(lambda jh=jh, c7=c7: cp(V("offL", 32 * b + jh, 32 * b + 32, 2), V("tp", c7, c7 + 16)))
         return L
 
     iota(V("pint", 0, 1), [[0, 1]], 0, 1, False)
@@ -251,11 +256,12 @@ def rank_program(g, core, T, topo):
     iota(V("c2", 320, 326), [[16, 6]], 32)
     iota(V("lowc", 0, 112), [[16, 14], [1, 8]])
     iota(V("lowc", 112, 224), [[16, 14], [1, 8]])
+    iota(V("D", P0 + O, P0 + O + 1920), [[0, 1920]])
     iota(V("ci", 0, 256), [[0, 16], [2, 16]])
     iota(V("ci", 256, 512), [[0, 16], [2, 16]], 1)
     iota(V("ci", 512, 768), [[1, 16], [100, 2], [0, 8]])
-    iota(V("D", P0 + O, SB), [[0, P0 + O]])
     ms(V("D", 0, P0), 0.0)
+    ms(V("D", P0 + O + 1920, SB), 0.0)
     ms(V("NN", 0, P0), 0.0)
     ms(V("mo", 0, 10 * MS), 0)
     ms(V("c4", 0, 2), 65536.0)
@@ -272,34 +278,32 @@ def rank_program(g, core, T, topo):
     ts(C(3), C(2), 16.0, mul, 15.0, add)
     ts(C(5), C(1), 16.0, mul)
     ts(C(6), C(1), 16.0, mul, 256.0, add)
-    ts(V("identf", 0, 128), V("c2", 0, 128), C(0), eq)
-    ts(V("identb", 0, 128), V("c2", 0, 128), C(0), eq)
-    ts(V("Zp", 0, 144), V("c2", 0, 144), C(3), eq, WT, mul)
-    ts(V("Zn", 0, 144), V("c2", 0, 144), C(3), eq, -WT, mul)
     ts(V("qq", 0, 96), V("pi", 0, 96), float(P0), add)
     ts(V("ff", 96, 192), V("ff", 0, 96), -1.0, mul)
-    act(V("fexp", 0, 1536), I(V("ff", 0, 96), V("oc", 0, 96)), AF.Copy)
+    act(V("fexp", 0, 512), I(V("ff", 0, 96), V("oc", 0, 32)), AF.Copy)
     act(V("delta", 0, 288), I(V("ff", 0, 192), V("oc", 96, 114)), AF.Copy)
-    more = [lambda: ts(V("i16", 0, 48), V("c2", 272, 320), C(1), eq),
+    act(V("fexp", 512, 1536), I(V("ff", 0, 96), V("oc", 32, 96)), AF.Copy)
+    more = [lambda: ts(V("identb", 0, 128), V("c2", 0, 128), C(0), eq),
+            lambda: ts(V("Zp", 0, 144), V("c2", 0, 144), C(3), eq, WT, mul),
+            lambda: ts(V("Zn", 0, 144), V("c2", 0, 144), C(3), eq, -WT, mul),
+            lambda: ts(V("i16", 0, 48), V("c2", 272, 320), C(1), eq),
             lambda: ts(V("nn", 0, 48), V("c2", 272, 320), C(1), gt),
             lambda: ts(V("cscan", 0, 48), V("c2", 272, 320), C(1), neq),
             lambda: ts(V("tr", 0, 6), V("c2", 320, 326), C(1), add),
             lambda: tt(V("nn", 0, 48), V("i16", 0, 48), V("nn", 0, 48), sub),
             lambda: ms(V("lowc", 96, 97), 232.0 - WT),
             lambda: ms(V("lowc", 112 + 104, 112 + 105), 232.0 - WT),
-            lambda: ts(V("maskT", 0, 48), V("nn", 0, 48), BIG, mul)]
-    for f in prep_ops(0, "v") + prep_ops(1, "v") + prep_ops(2, "v"):
-        if more and peek(f)[0] > 40:
-            more.pop(0)()
-        f()
-    for f in more:
-        f()
-    ts(V("MW", 0, 768), V("ci", 0, 768), C(1), eq)
-    ts(V("detf", 0, h), V("dets", 0, h), float(P0), add)
+            lambda: ts(V("maskT", 0, 48), V("nn", 0, 48), BIG, mul),
+            lambda: ts(V("identf", 0, 128), V("c2", 0, 128), C(0), eq)]
+    for k, fs in enumerate(zip(*[prep_ops(z, "v", z) for z in range(2)])):
+        for f in fs + tuple(more[k - 4:k - 3] if k >= 4 else ()):
+            f()
     ts(V("abf", 0, 512), I(V("dets", 0, O), V("site", 0, 32)), float(P0), add)
-    ts(V("detf", h, O), V("dets", h, O), float(P0), add)
+    ts(V("detf", 0, 704), V("dets", 0, 704), float(P0), add)
     cp(V("ab16", 0, 512), V("abf", 0, 512))
-    act(V("NN", P0 + O, P0 + W), V("D", SB, SB + S), AF.Relu, None, -1.0)
+    hb = S - 640
+    act(V("NN", P0 + O, P0 + O + hb), V("D", SB, SB + hb), AF.Relu, None, -1.0)
+    ts(V("NN", P0 + O + hb, P0 + W), V("D", SB + hb, SB + S), -1.0, mul, 0.0, mx)
     act(V("NN", P0, P0 + h), V("D", P0, P0 + h), AF.Relu, None, -1.0)
     ts(V("NN", P0 + h, P0 + h2), V("D", P0 + h, P0 + h2), -1.0, mul, 0.0, mx)
     hh = P0 + h2 + 256
@@ -327,13 +331,13 @@ def rank_program(g, core, T, topo):
                 mm(V("PB", 64 + 32 * k, 96 + 32 * k), blk, V("ncd", 0, 32), True, True)
             act(V("WW", 64 * b, 64 * b + 32), V("PC", 32, 64), AF.Sign)
         L = [lambda: ts(V("ncd", 0, 16), V("i16", 0, 16), ncol(0), mul), spread]
-        L2 = [lambda: ts(tp(10, 2), V("PB", 0, 64), float(P0 + O), ge, float(B * S), mul),
-              lambda: tt(tp(12, 2), V("WW", 64 * b, 64 * b + 64), V("PB", 64, 128), mul),
-              lambda: tt(tp(10, 2), tp(10, 2), V("PB", 0, 64), add),
-              lambda: tt(tp(10), tp(10), q, sub),
-              lambda: tt(tp(10, 2), tp(10, 2), tp(12, 2), mul),
-              lambda: tt(q, q, tp(10), add),
-              lambda: tt(q, q, tp(11), mx)]
+        L2 = [lambda: ts(tq(10, 2), V("PB", 0, 64), float(P0 + O), ge, float(B * S), mul),
+              lambda: tt(tq(12, 2), V("WW", 64 * b, 64 * b + 64), V("PB", 64, 128), mul),
+              lambda: tt(tq(10, 2), tq(10, 2), V("PB", 0, 64), add),
+              lambda: tt(tq(10), tq(10), q, sub),
+              lambda: tt(tq(10, 2), tq(10, 2), tq(12, 2), mul),
+              lambda: tt(q, q, tq(10), add),
+              lambda: tt(q, q, tq(11), mx)]
         if t >= 3:
             L2.append(lambda: aff(V("ypo", 32 * b, 32 * b + 32), q, 1.0, float(-P0), "v" if t == ST - 1 else "a"))
         return L, L2
@@ -435,8 +439,10 @@ def rank_program(g, core, T, topo):
                 pass
             f()
 
-    spill = []
+    spill = prep_ops(2)
     head = []
+    Lx = [lambda: ts(V("MW", 0, 768), V("ci", 0, 768), C(1), eq)]
+    Lx += [lambda c=c: ts(V("detf", c, c + 352), V("dets", c, c + 352), float(P0), add) for c in range(704, O, 352)]
     bulk(0)
     for t in range(ST):
         b = t % 3
@@ -484,7 +490,7 @@ def rank_program(g, core, T, topo):
         Lv = head + [lambda: tt(V("XL", 0, 512), I(V("D", 0, slot(t) + S), V("offL", 32 * b, 32 * b + 32)), V("fexp", 512 * b, 512 * b + 512), mn), lrelu]
         La = [lcopy]
         flows = list(range(32))
-        while flows or Lv or La or t0:
+        while flows or Lv or La or t0 or Lx:
             a_on = flows or (La and not Lv)
             if a_on and clock["a"] <= clock["v"]:
                 if La and not Lv and (not flows or peek(La[0])[0] < 40):
@@ -492,7 +498,7 @@ def rank_program(g, core, T, topo):
                 else:
                     flow(flows.pop(0), "a")
                 continue
-            ch = Lv or (t0 if left[0] == 0 else [])
+            ch = Lv or Lx or (t0 if left[0] == 0 else [])
             gap = peek(ch[0])[0] if ch else 1e9
             if ch and (gap < 40 or peek(ch[0])[2] != "v"):
                 ch.pop(0)()

from concourse.mybir import AluOpType, AxisListType, ActivationFunctionType

O, S, FB, ST, NR = 2816, 2048, 32, 6, 4
W = O + S
P0 = 128
SB = 2 * (P0 + O)
DW = SB + ST * S
BIG = 8192.0
WT = 1024.0
XS = 208
MS = 56

SCRATCH = {
    "D": ("sbuf", [128, DW], "bfloat16"), "NN": ("sbuf", [128, DW], "float32"),
    "dets": ("sbuf", [128, O], "int32"), "detf": ("sbuf", [128, O], "float32"),
    "pi": ("sbuf", [128, 96], "int32"), "ff": ("sbuf", [128, 192], "bfloat16"),
    "qq": ("sbuf", [128, 96], "float32"), "ypo": ("sbuf", [128, 96], "float32"),
    "X": ("sbuf", [128, 32 * XS], "bfloat16"), "XL": ("sbuf", [128, 512], "bfloat16"),
    "fexp": ("sbuf", [128, 1536], "bfloat16"), "delta": ("sbuf", [128, 288], "bfloat16"),
    "abf": ("sbuf", [128, 1536], "float32"), "ab16": ("sbuf", [128, 1536], "uint16"),
    "GG": ("sbuf", [128, 288], "float32"), "offL": ("sbuf", [128, 96], "uint16"), "site": ("sbuf", [128, 96], "uint16"),
    "WW": ("sbuf", [128, 192], "float32"), "tp": ("sbuf", [128, 1088], "float32"),
    "ci": ("sbuf", [128, 768], "float32"), "c2": ("sbuf", [128, 464], "float32"), "pint": ("sbuf", [128, 8], "int32"),
    "col": ("sbuf", [128, 16], "float32"),
    "identf": ("sbuf", [128, 128], "float32"), "identb": ("sbuf", [128, 128], "bfloat16"), "blockf": ("sbuf", [128, 128], "float32"),
    "Zp": ("sbuf", [128, 144], "bfloat16"), "Zn": ("sbuf", [128, 144], "bfloat16"),
    "maskT": ("sbuf", [128, 48], "bfloat16"), "cscan": ("sbuf", [128, 48], "float32"), "i16": ("sbuf", [128, 48], "float32"),
    "MW": ("sbuf", [128, 768], "float32"), "lowc": ("sbuf", [128, 224], "bfloat16"),
    "oc": ("sbuf", [128, 144], "uint16"), "tr": ("sbuf", [128, 8], "bfloat16"), "c4": ("sbuf", [128, 4], "float32"),
    "Lsb": ("sbuf", [128, 32], "bfloat16"),
    "key": ("sbuf", [128, 8], "float32"), "u": ("sbuf", [128, 16], "int32"), "o16": ("sbuf", [128, 32], "uint16"),
    "M": ("sbuf", [128, 96], "float32"), "XO": ("sbuf", [128, 96], "float32"), "ne": ("sbuf", [128, 288], "bfloat16"),
    "ns": ("sbuf", [128, 288], "bfloat16"), "nn": ("sbuf", [128, 96], "float32"),
    "ndf": ("sbuf", [128, 576], "float32"), "rd": ("sbuf", [128, 480], "float32"),
    "yy": ("sbuf", [128, 32], "float32"), "ncd": ("sbuf", [128, 32], "float32"), "oo": ("sbuf", [128, 8], "uint16"),
    "mo": ("sbuf", [128, 10 * MS], "uint16"), "lo": ("sbuf", [128, 10 * MS], "uint16"),
    "S0": ("psum", [128, 512], "float32"), "S1": ("psum", [128, 512], "float32"), "PL": ("psum", [128, 512], "float32"),
    "NA": ("psum", [128, 512], "float32"), "NB": ("psum", [128, 512], "float32"), "PB": ("psum", [128, 512], "float32"),
    "PC": ("psum", [128, 512], "float32"),
}
PSUM = ("S0", "S1", "PL", "NA", "NB", "PB", "PC")
SEMAPHORES = (["qv", "qa", "qp", "qg", "ml"] + ["ld%d" % k for k in range(8)] + ["st%d" % k for k in range(3)]
              + ["ba%d" % k for k in range(5)] + ["ma%d" % k for k in range(10)] + ["md%d" % k for k in range(10)]
              + ["bl%d" % k for k in range(5)])

PL = {"cyc": 0.9, "gat": 1.4, "sca": 3.5, "pe": 0.45, "lat": 140.0, "rem": 2000.0, "bw": 250.0, "cut": 11}
add, sub, mul, mx, mn = AluOpType.add, AluOpType.subtract, AluOpType.mult, AluOpType.max, AluOpType.min
eq, neq, ge, gt = AluOpType.is_equal, AluOpType.not_equal, AluOpType.is_ge, AluOpType.is_gt
AF = ActivationFunctionType


def rank_program(g, core, T, topo):
    r = T.rank_of(core)
    if r is None:
        return
    Q = {"v": g.vector, "a": g.scalar, "p": g.tensor, "g": g, "s": g.sync}
    cnt = {"qv": 0, "qa": 0, "qp": 0, "qg": 0}
    known = {q: {} for q in Q}
    clock = {q: 0.0 for q in Q}
    clock["dma"] = 0.0
    hist = {}
    final = {}
    dry = []

    def V(name, lo, hi, step=1):
        return (T[name][:, lo:hi:step] if step > 1 else T[name][:, lo:hi], [(name, lo, hi, -(-(hi - lo) // step))])

    def I(win, off):
        return (win[0].indirect(off[0]), win[1], off[1])

    def ap(x):
        return x[0] if isinstance(x, tuple) else x

    def wide(x):
        return 2 if SCRATCH[x[1][0][0]][2] in ("bfloat16", "uint16") else 4

    def cost(o, i, k=1.0, fix=50.0):
        if len(o) == 3:
            return fix + 16 * o[2][0][3] * PL["sca"] * PL["cyc"]
        if len(i) == 3:
            return fix + 16 * i[2][0][3] * PL["gat"] * PL["cyc"]
        return max(64, i[1][0][3] * k * (0.5 if wide(o) + wide(i) == 4 and fix == 50.0 else 1)) * PL["cyc"]

    def note(q, tk, rd, wr):
        for lst, w in ((rd, False), (wr, True)):
            for nm, lo, hi, n in lst:
                h = hist.setdefault(nm, [])
                if w:
                    h[:] = [e for e in h if not (lo <= e[0] and e[1] <= hi and nm not in PSUM)]
                h[:] = [e for e in h if not (e[4] == q and e[3][0] == tk[0] and lo <= e[0] and e[1] <= hi and (w or not e[2]))]
                h.append((lo, hi, w, tk, q))
        final[tk[0]] = max(final.get(tk[0], 0), tk[1])

    def op(q, fn, ins, outs, c, sem=None, inc=1, extra=()):
        rd, wr = [], []
        for x in ins:
            if isinstance(x, tuple):
                for part in x[1:]:
                    rd += part
        for x in outs:
            wr += x[1]
            for part in x[2:]:
                rd += part
        who = sem or q
        toks = list(extra)
        for lst, w in ((rd, False), (wr, True)):
            for nm, lo, hi, n in lst:
                for e in hist.get(nm, []):
                    if nm in PSUM and e[4] != who:
                        toks.append(e[3])
                    elif (w or e[2]) and lo < e[1] and e[0] < hi and not (who == "p" and e[4] == "p"):
                        toks.append(e[3])
        start = max([clock[q]] + [tk[3] + PL["lat"] for tk in toks if known[q].get(tk[0], 0) < tk[1]])
        if dry:
            dry[0] = (start - clock[q], c, q)
            raise StopIteration
        for tk in sorted(toks, key=lambda z: -z[1]):
            if known[q].get(tk[0], 0) < tk[1]:
                Q[q].wait_ge(T.sem[tk[0]], tk[1])
                known[q][tk[0]] = tk[1]
                for k, v in tk[2].items():
                    if known[q].get(k, 0) < v:
                        known[q][k] = v
        if sem is None:
            sem = "q" + q
            cnt[sem] += 1
            clock[q] = start + c
            tk = (sem, cnt[sem], dict(known[q]), clock[q])
            fn().then_inc(T.sem[sem], 1)
        else:
            clock[q] = start + 100
            clock["dma"] = max(start + PL["rem"], clock["dma"]) + c
            tk = (sem, inc, dict(known[q]), clock["dma"])
            fn()
        note(who, tk, rd, wr)
        return tk

    def peek(f):
        dry.append(None)
        try:
            f()
        except StopIteration:
            pass
        return dry.pop()

    def ts(o, i, s1, op0, s2=None, op1=None):
        if op1 is None:
            return op("v", lambda: g.vector.tensor_scalar(o[0], i[0], ap(s1), None, op0), [i, s1], [o], cost(o, i))
        return op("v", lambda: g.vector.tensor_scalar(o[0], i[0], ap(s1), ap(s2), op0, op1), [i, s1, s2], [o], cost(o, i))

    def tt(o, a, b, f):
        return op("v", lambda: g.vector.tensor_tensor(o[0], a[0], b[0], f), [a, b], [o], cost(o, a, 2.0))

    def cp(o, i):
        return op("v", lambda: g.vector.tensor_copy(o[0], i[0]), [i], [o], cost(o, i))

    def ms(o, c):
        return op("v", lambda: g.vector.memset(o[0], c), [], [o], cost(o, o))

    def red(o, i):
        return op("v", lambda: g.vector.tensor_reduce(o[0], i[0], AxisListType.X, mn), [i], [o], cost(o, i))

    def scan(o, d0, d1, ini, op0, op1):
        return op("v", lambda: g.vector.tensor_tensor_scan(o[0], d0[0], d1[0], ini, op0, op1), [d0, d1], [o], cost(o, d0))

    def act(o, i, f, bias=None, scale=1.0):
        if bias is None:
            return op("a", lambda: g.scalar.activation(o[0], i[0], f, scale=scale), [i], [o], cost(o, i, 1.0, 65.0))
        return op("a", lambda: g.scalar.activation(o[0], i[0], f, bias=ap(bias), scale=scale), [i, bias], [o], cost(o, i, 1.0, 65.0))

    def aff(o, i, a, c, on):
        return act(o, i, AF.Identity, c, a) if on == "a" else ts(o, i, a, mul, c, add)

    def mm(o, l, x, st, sp):
        return op("p", lambda: g.tensor.matmul(o[0], l[0], x[0], st, sp), [l, x], [o], max(64, x[1][0][3]) * PL["pe"] * (4 if wide(x) == 4 else 1))

    def iota(o, pat, base=0, cm=0, flt=True):
        c = 130 + 2 * o[1][0][3] * PL["cyc"]
        if flt:
            return op("g", lambda: g.iota(o[0], pat, base, cm, allow_small_or_imprecise_dtypes=True), [], [o], c)
        return op("g", lambda: g.iota(o[0], pat, base, cm), [], [o], c)

    def dma(q, sem, o, i):
        x = o if o[1] else i
        return op(q, lambda: Q[q].dma_start(o[0], i[0]).then_inc(T.sem[sem], 16), [i], [o], 128 * x[1][0][3] * wide(x) / PL["bw"], sem=sem, inc=16)

    def H(x):
        return (x, [])

    def slot(t):
        return SB + t * S

    def C(k):
        return V("col", k, k + 1)

    def tq(k, n=1):
        return V("tp", 32 * k, 32 * (k + n))

    nxt = T.cores[(r - 1) % NR]
    rid, pid = topo.addr(nxt)[0:2]
    ne_ = len(topo.engines(core, nxt))
    m_all = topo.mask(core, nxt)

    def send(src, dst, rsem, lsem, extra=()):
        tk = op("g", lambda: g.remote_dma(dst[0], src[0], T.sem[rsem], T.sem[lsem], pid, rid, m_all), [src], [],
                128 * src[1][0][3] * 2 / PL["bw"], sem=lsem, inc=final.get(lsem, 0) + ne_, extra=extra)
        note("rem", (rsem, ne_, {}, tk[3]), [], dst[1])

    h, h2 = O // 2, 2304
    dma("a", "ld0", V("pi", 0, 96), H(T.pth[:]))
    dma("s", "ld1", V("ff", 0, 96), H(T.fv[:]))
    dma("s", "ld2", V("dets", 0, O), H(T.det[:]))
    dma("s", "ld3", V("D", SB, SB + S), H(T.dn[:, O:W]))
    dma("s", "ld4", V("D", P0, P0 + h), H(T.dn[:, 0:h]))
    dma("s", "ld5", V("D", P0 + h, P0 + h2), H(T.dn[:, h:h2]))
    last_load = dma("s", "ld7", V("D", P0 + h2, P0 + O), H(T.dn[:, h2:O]))

    def prep_ops(t, on="a", z=0):
        b = t % 3
        B = (r + t) % NR
        q = V("qq", 32 * b, 32 * b + 32)
        sh = float(slot(t) - P0 - O)
        k0 = (0, 14, 24)[z]
        pc = V("PC", (0, 64, 96)[z], (0, 64, 96)[z] + 32)

        def tp(k):
            return tq(k0 + k)
        L = [lambda: aff(tp(0), q, 1.0, float(-B * S), on),
             lambda: act(tp(8), q, AF.Sign, float(1 - P0)) if on == "a" else ts(tp(8), q, float(P0), ge),
             lambda: ts(tp(2), q, float(P0), mx, float(P0 + O - 1), mn),
             lambda: mm(pc, V("blockf", 0, 128), tp(8), True, True),
             lambda: ts(tp(1), tp(0), float(P0 + O), mx, float(P0 + W - 1), mn),
             lambda: tt(tp(4), tp(2), q, eq),
             lambda: tt(tp(3), tp(1), tp(0), eq),
             lambda: tt(tp(2), tp(2), tp(4), mul),
             lambda: aff(tp(6), tp(3), float(-O), float(-P0), on),
             lambda: aff(tp(7), tp(3), sh, 0.0, on),
             lambda: tt(tp(1), tp(1), tp(3), mul),
             lambda: ts(V("WW", 64 * b + 32, 64 * b + 64), pc, C(1), eq),
             lambda: tt(tp(5), tp(1), tp(2), add),
             lambda: tt(tp(6), tp(6), tp(5), add),
             lambda: tt(tp(7), tp(7), tp(5), add),
             lambda: cp(V("site", 32 * b, 32 * b + 32), tp(6))]
        for jh in range(2):
            c5, c7 = 32 * (k0 + 5) + 16 * jh, 32 * (k0 + 7) + 16 * jh
            L.append(lambda jh=jh, c5=c5: aff(V("GG", 96 * b + 48 * jh + 32, 96 * b + 48 * jh + 48), V("tp", c5, c5 + 16), 1.0, 0.0, "a"))
            L.append(lambda jh=jh, c7=c7: cp(V("offL", 32 * b + jh, 32 * b + 32, 2), V("tp", c7, c7 + 16)))
        return L

    iota(V("pint", 0, 1), [[0, 1]], 0, 1, False)
    iota(V("c2", 144, 272), [[1, 8], [0, 16]])
    iota(V("c2", 336, 432), [[32, 3], [1, 16], [16, 2]])
    iota(V("c2", 432, 450), [[16, 6], [0, 3]])
    iota(V("c2", 0, 144), [[1, 144]])
    iota(V("c2", 272, 320), [[0, 3], [1, 16]])
    iota(V("c2", 320, 326), [[16, 6]], 32)
    iota(V("lowc", 0, 112), [[16, 14], [1, 8]])
    iota(V("lowc", 112, 224), [[16, 14], [1, 8]])
    iota(V("D", P0 + O, P0 + O + 1920), [[0, 1920]])
    iota(V("ci", 0, 256), [[0, 16], [2, 16]])
    iota(V("ci", 256, 512), [[0, 16], [2, 16]], 1)
    iota(V("ci", 512, 768), [[1, 16], [100, 2], [0, 8]])
    ms(V("D", 0, P0), 0.0)
    ms(V("D", P0 + O + 1920, SB), 0.0)
    ms(V("NN", 0, P0), 0.0)
    ms(V("mo", 0, 10 * MS), 0)
    ms(V("c4", 0, 2), 65536.0)
    ms(V("c4", 2, 3), 65536.0 + 256)
    ms(V("c4", 3, 4), 65536.0 + 512)
    cp(C(0), V("pint", 0, 1))
    ts(V("pint", 1, 2), V("pint", 0, 1), 15, AluOpType.bitwise_and)
    ts(V("pint", 2, 3), V("pint", 0, 1), 4, AluOpType.arith_shift_right)
    cp(V("oc", 0, 96), V("c2", 336, 432))
    cp(V("col", 1, 3), V("pint", 1, 3))
    ts(V("c2", 434, 450, 3), V("c2", 434, 450, 3), 96.0, add)
    ts(V("blockf", 0, 128), V("c2", 144, 272), C(2), eq)
    ts(V("oc", 96, 114), V("c2", 432, 450), C(1), add)
    ts(C(3), C(2), 16.0, mul, 15.0, add)
    ts(C(5), C(1), 16.0, mul)
    ts(C(6), C(1), 16.0, mul, 256.0, add)
    ts(V("qq", 0, 96), V("pi", 0, 96), float(P0), add)
    ts(V("ff", 96, 192), V("ff", 0, 96), -1.0, mul)
    act(V("fexp", 0, 512), I(V("ff", 0, 96), V("oc", 0, 32)), AF.Copy)
    act(V("delta", 0, 288), I(V("ff", 0, 192), V("oc", 96, 114)), AF.Copy)
    act(V("fexp", 512, 1536), I(V("ff", 0, 96), V("oc", 32, 96)), AF.Copy)
    more = [lambda: ts(V("identb", 0, 128), V("c2", 0, 128), C(0), eq),
            lambda: ts(V("Zp", 0, 144), V("c2", 0, 144), C(3), eq, WT, mul),
            lambda: ts(V("Zn", 0, 144), V("c2", 0, 144), C(3), eq, -WT, mul),
            lambda: ts(V("i16", 0, 48), V("c2", 272, 320), C(1), eq),
            lambda: ts(V("nn", 0, 48), V("c2", 272, 320), C(1), gt),
            lambda: ts(V("cscan", 0, 48), V("c2", 272, 320), C(1), neq),
            lambda: ts(V("tr", 0, 6), V("c2", 320, 326), C(1), add),
            lambda: tt(V("nn", 0, 48), V("i16", 0, 48), V("nn", 0, 48), sub),
            lambda: ms(V("lowc", 96, 97), 232.0 - WT),
            lambda: ms(V("lowc", 112 + 104, 112 + 105), 232.0 - WT),
            lambda: ts(V("maskT", 0, 48), V("nn", 0, 48), BIG, mul),
            lambda: ts(V("identf", 0, 128), V("c2", 0, 128), C(0), eq)]
    for k, fs in enumerate(zip(*[prep_ops(z, "v", z) for z in range(2)])):
        for f in fs + tuple(more[k - 4:k - 3] if k >= 4 else ()):
            f()
    ts(V("abf", 0, 512), I(V("dets", 0, O), V("site", 0, 32)), float(P0), add)
    ts(V("detf", 0, 704), V("dets", 0, 704), float(P0), add)
    cp(V("ab16", 0, 512), V("abf", 0, 512))
    hb = S - 640
    act(V("NN", P0 + O, P0 + O + hb), V("D", SB, SB + hb), AF.Relu, None, -1.0)
    ts(V("NN", P0 + O + hb, P0 + W), V("D", SB + hb, SB + S), -1.0, mul, 0.0, mx)
    act(V("NN", P0, P0 + h), V("D", P0, P0 + h), AF.Relu, None, -1.0)
    ts(V("NN", P0 + h, P0 + h2), V("D", P0 + h, P0 + h2), -1.0, mul, 0.0, mx)
    hh = P0 + h2 + 256
    act(V("NN", P0 + h2, hh), V("D", P0 + h2, hh), AF.Relu, None, -1.0)
    ts(V("NN", hh, P0 + O), V("D", hh, P0 + O), -1.0, mul, 0.0, mx)

    def ncol(jh):
        k = 144 * jh + (71 if jh == 0 else 143)
        return V("ns", k, k + 1)

    def path_ops(t):
        b = t % 3
        B = (r + t) % NR
        q = V("qq", 32 * b, 32 * b + 32)
        blk = V("blockf", 0, 128)

        def spread():
            ts(V("ncd", 16, 32), V("i16", 0, 16), ncol(1), mul)
            for jh in range(2):
                mm(V("PC", 32 + 16 * jh, 48 + 16 * jh), V("identf", 0, 128), V("M", 48 * jh + 32, 48 * jh + 48), True, True)
            for ty in range(2):
                for jh in range(2):
                    mm(V("PB", 32 * ty + 16 * jh, 32 * ty + 16 * jh + 16), blk, V("M", 48 * jh + 16 * ty, 48 * jh + 16 * ty + 16), True, True)
            for k in range(2):
                mm(V("PB", 64 + 32 * k, 96 + 32 * k), blk, V("ncd", 0, 32), True, True)
            act(V("WW", 64 * b, 64 * b + 32), V("PC", 32, 64), AF.Sign)
        L = [lambda: ts(V("ncd", 0, 16), V("i16", 0, 16), ncol(0), mul), spread]
        L2 = [lambda: ts(tq(10, 2), V("PB", 0, 64), float(P0 + O), ge, float(B * S), mul),
              lambda: tt(tq(12, 2), V("WW", 64 * b, 64 * b + 64), V("PB", 64, 128), mul),
              lambda: tt(tq(10, 2), tq(10, 2), V("PB", 0, 64), add),
              lambda: tt(tq(10), tq(10), q, sub),
              lambda: tt(tq(10, 2), tq(10, 2), tq(12, 2), mul),
              lambda: tt(q, q, tq(10), add),
              lambda: tt(q, q, tq(11), mx)]
        if t >= 3:
            L2.append(lambda: aff(V("ypo", 32 * b, 32 * b + 32), q, 1.0, float(-P0), "v" if t == ST - 1 else "a"))
        return L, L2

    def tail_ops(t, jh):
        b = t % 3
        R = 12 if t < 3 else 13
        sh = float(slot(t) - P0 - O)
        bank, c0, wd = ("NA", 0, 48) if jh == 0 else ("NB", 48, 96)
        key = V("key", jh, jh + 1)
        nc = ncol(jh)
        u = V("u", 8 * jh, 8 * jh + 4)
        oS, oK, oD = V("o16", 16 * jh, 16 * jh + 2), V("o16", 16 * jh + 4, 16 * jh + 7), V("o16", 16 * jh + 8, 16 * jh + 11)
        g0 = 96 * b + 48 * jh
        Mv = V("M", 48 * jh, 48 * jh + 48)
        x = V("XO", 48 * jh + 15, 48 * jh + 48, 16)
        y0 = 16 * jh
        mk, y, ym = V("yy", y0, y0 + 3), V("yy", y0 + 4, y0 + 7), V("yy", y0 + 8, y0 + 11)
        n0 = 96 * t + 48 * jh
        nD = V("ndf", n0, n0 + 48)
        m0 = MS * (2 * t + jh)
        hw = 3 * wd // 2

        def names():
            tt(Mv, I(V("MW", 0, 768), oK), V("GG", g0, g0 + 48), mul)
            mm(V(bank, c0, c0 + 48), V("blockf", 0, 128), Mv, False, True)
            if jh == 0:
                mm(V("NB", 0, 48), V("blockf", 0, 128), Mv, True, True)
                mm(V("NB", 48, 96), V("identb", 0, 128), V("maskT", 0, 48), True, False)

        def cmp_(c):
            xc = V("XO", 48 * jh + 16 * c + 15, 48 * jh + 16 * c + 16)
            return lambda: ts(V("ne", wd * c, wd * c + wd), V(bank, 0, wd), BIG, add, xc, neq)
        L = [lambda: red(key, V("S%d" % jh, 0, 8 * R + 1)),
             lambda: ts(u, V("c4", 0, 4), key, add),
             lambda: ts(V("u", 8 * jh + 4, 8 * jh + 8), u, 1023, AluOpType.bitwise_and),
             lambda: ts(oS, V("u", 8 * jh + 4, 8 * jh + 6), 1.0 / 16, mul, C(5 + jh), add),
             lambda: cp(oK, V("u", 8 * jh + 5, 8 * jh + 8)),
             lambda: cp(V("GG", g0, g0 + 32), I(V("abf", 512 * b, 512 * b + 512), oS)),
             names,
             lambda: scan(V("XO", 48 * jh, 48 * jh + 48), V("cscan", 0, 48), V(bank, c0, c0 + 48), 0.0, mul, mx),
             lambda: ts(mk, x, P0 + O + BIG, ge, sh, mul),
             cmp_(0),
             cmp_(1),
             lambda: tt(y, x, mk, add),
             cmp_(2),
             lambda: ts(oD, y, -BIG, add),
             lambda: scan(V("ns", 144 * jh, 144 * jh + hw), V("ne", 0, hw), V("ne", hw, 2 * hw), 1.0, mn, mn),
             lambda: tt(nD, I(V("D", 0, slot(t) + S), oD), V("delta", g0, g0 + 48), add)]
        own = []
        for c in range(3):
            k = 3 * jh + c
            ko = k if t < ST - 1 else 4 * jh + c
            own.append(lambda c=c, k=k, ko=ko: ts(V("oo", ko, ko + 1), V("o16", 16 * jh + 8 + c, 16 * jh + 9 + c), nc, mul, V("tr", k, k + 1), mx))
        if t == ST - 1:
            return L + own + [lambda: cp(I(V("D", 0, slot(t) + S), V("oo", 4 * jh, 4 * jh + 3)), nD)], []
        L.insert(14, lambda: ts(ym, y, -BIG - sh, add))
        for c in range(3):
            k = 3 * jh + c
            L.append(lambda c=c, k=k: ts(V("mo", m0 + c, m0 + c + 1), V("yy", y0 + 8 + c, y0 + 9 + c), nc, mul, V("tr", k, k + 1), mx))
        L.append(lambda: ts(V("mo", m0 + 8, m0 + 56), nD, -1.0, mul))
        L.append(lambda: (send(V("mo", m0, m0 + MS), V("lo", m0, m0 + MS), "ma%d" % (2 * t + jh), "ml"),
                          send(nD, V("rd", n0, n0 + 48), "md%d" % (2 * t + jh), "ml")))
        return L, own

    def take(t, jh):
        m0 = MS * (2 * t + jh)
        n0 = 96 * t + 48 * jh
        off = V("lo", m0, m0 + 3)
        return [lambda: cp(I(V("NN", 0, P0 + W), off), V("lo", m0 + 8, m0 + 56)),
                lambda: cp(I(V("D", slot(t + 1) - P0 - O, slot(t + 1) + S), off), V("rd", n0, n0 + 48))]

    def bulk(t):
        if t < ST - 1:
            send(V("D", slot(t), slot(t) + S), V("D", slot(t + 1), slot(t + 1) + S), "ba%d" % t, "bl%d" % t, [last_load])

    def detours(t):
        b = t % 3
        act(V("abf", 512 * b, 512 * b + 512), I(V("detf", 0, O), V("site", 32 * b, 32 * b + 32)), AF.Copy)

    def narrow(t):
        c0 = 512 * (t % 3)
        return [lambda c=c: cp(V("ab16", c, c + 128), V("abf", c, c + 128)) for c in range(c0, c0 + 512, 128)]

    def fill(gap, lists):
        for l in lists:
            while l and peek(l[0])[2] != "v":
                l.pop(0)()
            if l:
                w, c, q = peek(l[0])
                if w + c <= gap + 40:
                    l.pop(0)()
                    return True
        return False

    def chain(fs, lists):
        for f in fs:
            while peek(f)[2] == "v" and peek(f)[0] > 30 and fill(peek(f)[0], lists):
                pass
            f()

    spill = prep_ops(2)
    head = []
    Lx = [lambda: ts(V("MW", 0, 768), V("ci", 0, 768), C(1), eq)]
    Lx += [lambda c=c: ts(V("detf", c, c + 352), V("dets", c, c + 352), float(P0), add) for c in range(704, O, 352)]
    bulk(0)
    for t in range(ST):
        b = t % 3
        R = 12 if t < 3 else 13
        left = [41, 41]
        lowv = V("lowc", 0 if R == 12 else 112, 112 if R == 12 else 224)

        def smm(jh, n, l, x, k=0, st=1):
            left[jh] -= 1
            mm(V("S%d" % jh, k, n, st), l, x, left[jh] == 40, left[jh] == 0)

        def flow(j, q):
            jh, j16 = divmod(j, 16)
            o = V("X", XS * j, XS * j + 16 * R)
            i = I(V("NN", 0, P0 + W), V("ab16", 512 * b + 16 * j, 512 * b + 16 * j + R))
            f = V("ff", 32 * b + j, 32 * b + j + 1)
            if q == "a":
                act(o, i, AF.Relu, f, -1.0)
            else:
                ts(o, i, f, sub, 0.0, mn)
            z = V("Zp" if q == "a" else "Zn", 15 - j16, 143 - j16)
            for e in range(2):
                smm(jh, 8 * R, z, V("X", XS * j + e, XS * j + 16 * R, 2))

        for jh in range(2):
            smm(jh, 112, V("identb", 0, 128), lowv)
        mm(V("NA", 0, 48), V("identb", 0, 128), V("maskT", 0, 48), True, False)

        def lrelu():
            ts(V("XL", 0, 512), V("XL", 0, 512), 0.0, mx)
            for j16 in range(16):
                mm(V("PL", 0, 32), V("Zn", 15 - j16, 143 - j16), V("XL", 32 * j16, 32 * j16 + 32), j16 == 0, j16 == 15)

        def lcopy():
            act(V("Lsb", 0, 32), V("PL", 0, 32), AF.Copy)
            for jh in range(2):
                for k in range(8):
                    smm(jh, 8 * R, V("identb", 0, 128), V("Lsb", 16 * jh, 16 * jh + R), k, 8)

        fv_ = 50 + 16 * R * PL["gat"] * PL["cyc"]
        t0, t0b = tail_ops(t, 0)
        t1, t1b = tail_ops(t, 1)
        t0x = t0[PL["cut"]:]
        t0 = t0[:PL["cut"]]
        Lv = head + [lambda: tt(V("XL", 0, 512), I(V("D", 0, slot(t) + S), V("offL", 32 * b, 32 * b + 32)), V("fexp", 512 * b, 512 * b + 512), mn), lrelu]
        La = [lcopy]
        flows = list(range(32))
        while flows or Lv or La or t0 or Lx:
            a_on = flows or (La and not Lv)
            if a_on and clock["a"] <= clock["v"]:
                if La and not Lv and (not flows or peek(La[0])[0] < 40):
                    La.pop(0)()
                else:
                    flow(flows.pop(0), "a")
                continue
            ch = Lv or Lx or (t0 if left[0] == 0 else [])
            gap = peek(ch[0])[0] if ch else 1e9
            if ch and (gap < 40 or peek(ch[0])[2] != "v"):
                ch.pop(0)()
                continue
            take_flow = flows and (flows[0] < 16 or clock["v"] + fv_ + 75 * len(t0) <= clock["a"] + (fv_ + 15) * len(flows))
            if take_flow and gap > 0.45 * fv_:
                flow(flows.pop(0), "v")
            elif fill(min(gap, 200), [spill]):
                pass
            elif take_flow and gap > 60:
                flow(flows.pop(0), "v")
            elif ch:
                ch.pop(0)()
            elif a_on:
                clock["v"] = clock["a"] + 1
        p1, p2 = path_ops(t)
        if t == ST - 1:
            chain(t1[:8], [t0x, spill])
            chain(t0x[:], [])
            p1[0]()
            chain(t1[8:], [spill])
            dma("s", "st0", H(T.yd[:, 0:O]), V("D", P0, P0 + O))
            dma("a", "st1", H(T.yd[:, O:W]), V("D", slot(t), slot(t) + S))
            for f in spill + p1[1:] + p2:
                f()
            dma("s", "st2", H(T.yp[:]), V("ypo", 0, 96))
            break
        act(V("NN", P0 + O, P0 + W), V("D", slot(t + 1), slot(t + 1) + S), AF.Relu, None, -1.0)
        if t == 0:
            detours(1)
        k0, k1 = take(t, 0), take(t, 1)
        g1, g2 = t0b + p1[0:1], narrow(t + 1)
        chain(t1[:9], [t0x, g2, spill] if t else [t0x, spill])
        chain(t0x[:], [])
        chain(t1[9:], [g2, g1, spill] if t else [g1, spill])
        nD = V("ndf", 96 * t, 96 * t + 96)
        act(V("nn", 0, 96), nD, AF.Relu, None, -1.0)
        for f in g1 + t1b + p1[1:]:
            f()
        must = [lambda: cp(I(V("D", 0, slot(t) + S), V("oo", 0, 6)), nD),
                lambda: cp(I(V("NN", 0, slot(t) + S), V("oo", 0, 6)), V("nn", 0, 96)), k0[1], k0[0]]
        chain(must, [spill, g2, p2])
        chain(spill + g2, [p2])
        if t + 2 < ST:
            detours(t + 2)
        spill = p2 + (prep_ops(t + 3) if t + 3 < ST else [])
        while spill and fill(peek(k1[0])[0] - 100, [spill]):
            pass
        k1[0]()
        head = [lambda t=t, f=k1[1]: (f(), bulk(t + 1))]
    for sem, v in final.items():
        g.sync.wait_ge(T.sem[sem], v)
